import numpy as np
import ml_dtypes


def mxq(x, axis, fmt="e4m3"):
    dtype, down = {"e4m3": (ml_dtypes.float8_e4m3fn, 7), "e5m2": (ml_dtypes.float8_e5m2, 14)}[fmt]
    v = np.moveaxis(np.asarray(x, np.float32).astype(ml_dtypes.bfloat16).astype(np.float64), axis, -1)
    blocks = v.reshape(v.shape[:-1] + (-1, 32))
    amax = np.abs(blocks).max(-1, keepdims=True)
    byte = np.maximum(np.where(amax > 0, np.frexp(amax)[1] - 1 + 127, 0) - down, 1)
    scale = np.exp2(byte - 127.0)
    codes = (blocks / scale).astype(np.float32).astype(dtype).astype(np.float64)
    return np.moveaxis((codes * scale).reshape(v.shape), -1, axis)


WIDE = False


def mx_kscale(k):
    if not WIDE:
        return np.ones(k)
    levels = np.array([10, -10, 5, -5, 0])
    if k % 512:
        return np.exp2(np.random.permutation(np.resize(levels, k // 32))).repeat(32)
    a = np.empty((k // 512, 16))
    for p in range(k // 512):
        a[p, :8] = np.random.permutation(np.resize(levels, 8))
        for g in range(8):
            far = levels[np.abs(levels - a[p, g]) >= 10]
            a[p, g + 8] = far[np.random.randint(len(far))]
    return np.exp2(a.ravel()).repeat(32)


def f64(x):
    return np.asarray(x).astype(np.float64)


def striped(idx):
    return np.tile(idx.reshape(-1, 16).T, (8, 1)).astype(np.uint16)


def unstriped(offs):
    return offs[:16].T.reshape(-1).astype(np.int64)


def pack_weight(w):
    k, n = w.shape
    w = f64(np.asarray(w, np.float32).astype(ml_dtypes.bfloat16)).reshape(k // 32, 32, n)
    amax = np.abs(w).max(1)
    byte = np.clip(np.where(amax > 0, np.frexp(amax)[1] - 1 + 127 - 7, 1), 1, 254)
    scaled = (w * np.exp2(127.0 - byte)[:, None, :]).reshape(k, n).astype(np.float32)
    words = np.ascontiguousarray(scaled.reshape(k // 512, 128, 4, n).transpose(0, 1, 3, 2)).astype(ml_dtypes.float8_e4m3fn).view(np.uint8)
    return words, np.ascontiguousarray(byte.astype(np.uint8).reshape(k // 512, 16, n))


def unpack_weight(words, scales):
    g, p, n, _ = words.shape
    vals = np.ascontiguousarray(words).view(ml_dtypes.float8_e4m3fn).astype(np.float64) * np.repeat(np.exp2(scales.astype(np.float64) - 127.0), 8, axis=1)[..., None]
    return vals.transpose(0, 1, 3, 2).reshape(g * 512, n)


E2M1 = np.array([0.0, 0.5, 1.0, 1.5, 2.0, 3.0, 4.0, 6.0, -0.0, -0.5, -1.0, -1.5, -2.0, -3.0, -4.0, -6.0])


def pack_fp4(w):
    k, n = w.shape
    w = f64(np.asarray(w, np.float32).astype(ml_dtypes.bfloat16)).reshape(k // 32, 32, n)
    amax = np.abs(w).max(1)
    mant, ex = np.frexp(amax / 6.0)
    byte = np.clip(np.where(amax > 0, np.where(mant > 0.5, ex, ex - 1) + 127, 1), 1, 254)
    scaled = (w * np.exp2(127.0 - byte)[:, None, :]).reshape(k, n).astype(np.float32)
    c = np.ascontiguousarray(scaled.reshape(k // 512, 128, 4, n).transpose(0, 1, 3, 2)).astype(ml_dtypes.float4_e2m1fn).view(np.uint8) & 0xF
    words = (c[..., 0::2] | (c[..., 1::2] << 4)).reshape(k // 512, 128, 2 * n)
    return np.ascontiguousarray(words), np.ascontiguousarray(byte.astype(np.uint8).reshape(k // 512, 16, n))


def unpack_fp4(words, scales):
    g, _, n = scales.shape
    words = np.ascontiguousarray(words).reshape(g, 128, n, 2)
    nib = np.empty((g, 128, n, 4), np.uint8)
    nib[..., 0::2] = words & 0xF
    nib[..., 1::2] = words >> 4
    vals = E2M1[nib] * np.repeat(np.exp2(scales.astype(np.float64) - 127.0), 8, axis=1)[..., None]
    return vals.transpose(0, 1, 3, 2).reshape(g * 512, n)


def gelu(v):
    return 0.5 * v * (1.0 + np.tanh(np.sqrt(2.0 / np.pi) * (v + 0.044715 * v**3)))


K, T, S, H, N, U = 1024, 2048, 512, 512, 128, 1024


def setup_inputs():
    n = np.random.standard_normal
    s = mx_kscale(K)[:, None]
    u = mx_kscale(H)
    packed_xT = pack_weight(n((K, T)) * s)
    packed_w2 = pack_fp4(n((H, N)) / np.sqrt(H) / u[:, None])
    return {
        "x_words": packed_xT[0],
        "x_scales": packed_xT[1],
        "w1": (n((K, H)) / np.sqrt(K) / s * u).astype(np.float32),
        "w2_words": packed_w2[0],
        "w2_scales": packed_w2[1],
        "skip": (n((H, U)) * u[:, None]).astype(np.float32),
        "offs": striped(np.random.permutation(T)[:S]),
        "cell": striped(np.random.permutation(U)[:S]),
    }


def reference(x_words, x_scales, w1, w2_words, w2_scales, skip, offs, cell):
    xq = unpack_weight(x_words, x_scales)[:, unstriped(offs)]
    up = np.zeros((H, U))
    up[:, unstriped(cell)] = gelu(mxq(f64(w1), 0, "e4m3").T @ xq)
    z = up + f64(skip)
    return unpack_fp4(w2_words, w2_scales).T @ mxq(z, 0, "e4m3")

@@ -1,0 +1,231 @@
+from contextlib import ExitStack
+
+import concourse.mybir as mybir
+from concourse.masks import make_identity
+
+K, T, S, H, N, U = 1024, 2048, 512, 512, 128, 1024
+FLOPS = 2 * K * H * S + 2 * H * N * U
+
+F32 = mybir.dt.float32
+BF16 = mybir.dt.bfloat16
+I32 = mybir.dt.int32
+U32 = mybir.dt.uint32
+U16 = mybir.dt.uint16
+U8 = mybir.dt.uint8
+FP8X4 = mybir.dt.float8_e4m3fn_x4
+FP4X4 = mybir.dt.float4_e2m1fn_x4
+GELU = mybir.ActivationFunctionType.Gelu_apprx_tanh
+
+P = 128
+PASSES = K // 512
+HALF = S // 2
+CHUNK = 256
+CHUNKS = U // CHUNK
+
+
+def tile_picked_unet_gelu_p_kernel(
+    tc, x_words, x_scales, w1, w2_words, w2_scales, skip, offs, cell, out
+):
+    nc = tc.nc
+    with ExitStack() as ctx:
+        lists = ctx.enter_context(tc.tile_pool(name="lists", bufs=1))
+        sb = ctx.enter_context(tc.tile_pool(name="sb", bufs=1))
+        ps = ctx.enter_context(tc.psum_pool(name="ps", bufs=1))
+
+        def bank(b, name):
+            return ps.tile([P, 512], F32, name=name, tag="bank%d" % b)
+
+        offs_sb = lists.tile([P, S // 16], U16, name="offs_sb")
+        cell_sb = lists.tile([P, S // 16], U16, name="cell_sb")
+        xs = sb.tile([P, T], U8, name="xs", align_bytes=64)
+        nc.vector.memset(xs[:].bitcast(I32), 0)
+        nc.sync.dma_start(offs_sb[:], offs)
+        for q in range(4):
+            nc.sync.dma_start(xs[32 * q : 32 * q + 8, :].bitcast(I32), x_scales[:, 4 * q : 4 * q + 4, :].bitcast(I32))
+
+        w_rows = w1.rearrange("(g k j) (h c) -> h g k j c", g=PASSES, j=4, h=2)
+
+        def load_w(h, g):
+            raw = sb.tile([P, 4, 256], F32, name="wraw%d%d" % (h, g), tag="wraw%d%d" % (h, g), align_bytes=64)
+            nc.sync.dma_start(raw[:], w_rows[h, g])
+            return raw
+
+        skip_rows = skip.rearrange("(h p u e) v -> h u p e v", h=2, u=2, e=2)
+
+        def load_skip(h, u):
+            sk = sb.tile([P, U], F32, name="skip%d%d" % (h, u))
+            nc.sync.dma_start(sk[:], skip_rows[h, u])
+            return sk
+
+        wraw = {}
+        for g in range(PASSES):
+            wraw[0, g] = load_w(0, g)
+        xw = []
+        for g in range(PASSES):
+            t = sb.tile([P, T], U32, name="xw%d" % g, align_bytes=64)
+            nc.sync.dma_start(t[:].bitcast(I32), x_words[g].rearrange("p n t -> p (n t)").bitcast(I32))
+            xw.append(t)
+        nc.sync.dma_start(cell_sb[:], cell)
+        sk = {}
+        sk[0, 0] = load_skip(0, 0)
+        for g in range(PASSES):
+            wraw[1, g] = load_w(1, g)
+        sk[0, 1] = load_skip(0, 1)
+        sk[1, 0] = load_skip(1, 0)
+        sk[1, 1] = load_skip(1, 1)
+        w2w = sb.tile([P, 2 * N], U8, name="w2w", align_bytes=64)
+        w2s = sb.tile([P, N], U8, name="w2s", align_bytes=64)
+        nc.vector.memset(w2s[:].bitcast(I32), 0)
+        nc.sync.dma_start(w2w[:].bitcast(I32), w2_words[0].bitcast(I32))
+        for q in range(4):
+            nc.sync.dma_start(w2s[32 * q : 32 * q + 4, :].bitcast(I32), w2_scales[0, 4 * q : 4 * q + 4, :].bitcast(I32))
+
+        ident = sb.tile([P, P], F32, name="ident")
+        make_identity(nc, ident[:])
+        win = {}
+        for h in range(2):
+            for u in range(2):
+                win[h, u] = sb.tile([P, U], F32, name="win%d%d" % (h, u))
+                nc.vector.memset(win[h, u][:], 0.0)
+
+        wb, wc, ws = {}, {}, {}
+        for h in range(2):
+            for u in range(2):
+                wb[h, u] = sb.tile([P, PASSES * 512], BF16, name="wb%d%d" % (h, u), align_bytes=64)
+                wc[h, u] = sb.tile([P, PASSES * P], U32, name="wc%d%d" % (h, u), align_bytes=64)
+                ws[h, u] = sb.tile([P, PASSES * P], U8, name="ws%d%d" % (h, u), align_bytes=64)
+
+        def cast_w(copy, h, g, u):
+            src = wraw[h, g][:].rearrange("k j (q u e) -> k u q j e", u=2, e=2)[:, u]
+            dst = wb[h, u][:, 512 * g : 512 * (g + 1)].rearrange("k (q e j) -> k q j e", e=2, j=4)
+            copy(dst, src)
+
+        def quant_w(h, u):
+            nc.vector.quantize_mx(out=wc[h, u][:].bitcast(FP8X4), scales=ws[h, u][:], in_=wb[h, u][:])
+
+        for g in range(PASSES):
+            for u in range(2):
+                cast_w(nc.vector.tensor_copy, 0, g, u)
+        for u in range(2):
+            quant_w(0, u)
+
+        xsg = sb.tile([P, S], U8, name="xsg", align_bytes=64)
+        nc.vector.tensor_copy(xsg[:], xs[:].indirect(offs_sb[:]))
+        xg = [sb.tile([P, S], U32, name="xg%d" % g, align_bytes=64) for g in range(PASSES)]
+        nc.vector.tensor_copy(xg[0][:], xw[0][:].indirect(offs_sb[:]))
+        for a in range(2):
+            nc.vector.tensor_copy(xg[1][:, HALF * a : HALF * (a + 1)], xw[1][:].indirect(offs_sb[:, 16 * a : 16 * (a + 1)]))
+
+        def first_product(acc, h, u, g, cols):
+            nc.tensor.matmul_mx(
+                out=acc,
+                lhsT=wc[h, u][:, P * g : P * (g + 1)].bitcast(FP8X4),
+                lhsT_scale=ws[h, u][:, P * g : P * (g + 1)],
+                rhs=xg[g][:, cols].bitcast(FP8X4),
+                rhs_scale=xsg[4 * g : P, cols],
+                start=(g == 0),
+                stop=(g == PASSES - 1),
+            )
+
+        acc = {}
+        for a in range(2):
+            for u in range(2):
+                acc[a, u] = bank(6 * a + u, "acc%d%d" % (a, u))
+        for g in range(PASSES):
+            for a in range(2):
+                for u in range(2):
+                    first_product(acc[a, u][:, :HALF], 0, u, g, slice(HALF * a, HALF * (a + 1)))
+
+        ha = sb.tile([P, 2, HALF], F32, name="ha")
+        for u in range(2):
+            nc.scalar.activation(ha[:, u, :], acc[0, u][:, :HALF], GELU)
+        for u in range(2):
+            nc.vector.tensor_copy(win[0, u][:].indirect(cell_sb[:, 0:16]), ha[:, u, :])
+
+        for g in range(PASSES):
+            for u in range(2):
+                cast_w(nc.scalar.copy, 1, g, u)
+        for u in range(2):
+            quant_w(1, u)
+
+        hb = sb.tile([P, 2, HALF], F32, name="hb", tag="wraw11", align_bytes=64)
+        for u in range(2):
+            nc.scalar.activation(hb[:, u, :], acc[1, u][:, :HALF], GELU)
+        for u in range(2):
+            nc.vector.tensor_copy(win[0, u][:].indirect(cell_sb[:, 16:32]), hb[:, u, :])
+
+        hfull = {}
+        for u in range(2):
+            accb = bank(u, "accb%d" % u)
+            for g in range(PASSES):
+                first_product(accb[:], 1, u, g, slice(0, S))
+            hfull[u] = sb.tile([P, S], F32, name="hfull%d" % u)
+            nc.scalar.activation(hfull[u][:], accb[:], GELU)
+
+        zt = {}
+        for u in range(2):
+            for c in range(CHUNKS):
+                zt[u, c] = sb.tile([P, 2, 256], BF16, name="zt%d%d" % (u, c), align_bytes=64)
+
+        def turn_sum(h, u, banks, copies):
+            per_bank = 8 // len(banks)
+            tiles = [bank(b, "zT%d%d%d" % (h, u, b)) for b in banks]
+            for src, first in ((sk[h, u], True), (win[h, u], False)):
+                for vt in range(8):
+                    s = vt % per_bank
+                    nc.tensor.matmul(
+                        tiles[vt // per_bank][:, P * s : P * (s + 1)],
+                        src[:, P * vt : P * (vt + 1)],
+                        ident[:],
+                        is_transpose=True,
+                        start=(first and s == 0),
+                        stop=(not first and s == per_bank - 1),
+                    )
+            for c in range(CHUNKS):
+                s = (2 * c) % per_bank
+                src = tiles[2 * c // per_bank][:, P * s : P * (s + 2)].rearrange("v (s q) -> v s q", s=2)
+                copies[c](zt[u, c][:, :, P * h : P * (h + 1)], src)
+
+        on_scalar = [nc.scalar.copy] * CHUNKS
+        in_turn = [nc.scalar.copy, nc.vector.tensor_copy] * (CHUNKS // 2)
+
+        turn_sum(0, 0, (2, 3), on_scalar)
+        turn_sum(0, 1, (4, 5), on_scalar)
+        nc.vector.tensor_copy(win[1, 0][:].indirect(cell_sb[:]), hfull[0][:])
+        nc.vector.tensor_copy(win[1, 1][:].indirect(cell_sb[:]), hfull[1][:])
+        turn_sum(1, 0, (2, 3), on_scalar)
+
+        back = [bank(c, "back%d" % c) for c in range(CHUNKS)]
+
+        def turn_back(u, c):
+            for s in range(2):
+                nc.tensor.transpose(
+                    back[c][:, CHUNK * u + P * s : CHUNK * u + P * (s + 1)], zt[u, c][:, s, :].bitcast(F32), ident[:]
+                )
+
+        for c in range(CHUNKS):
+            turn_back(0, c)
+        turn_sum(1, 1, (4, 5, 6, 7), in_turn)
+        for c in range(CHUNKS):
+            turn_back(1, c)
+        for c in range(CHUNKS):
+            z = sb.tile([P, 4 * CHUNK], BF16, name="z%d" % c, align_bytes=64)
+            in_turn[c](
+                z[:].bitcast(F32).rearrange("p (v u) -> p v u", u=2), back[c][:].rearrange("p (u v) -> p v u", u=2)
+            )
+            zc = sb.tile([P, CHUNK], U32, name="zc%d" % c, align_bytes=64)
+            zs = sb.tile([P, CHUNK], U8, name="zs%d" % c, align_bytes=64)
+            nc.vector.quantize_mx(out=zc[:].bitcast(FP8X4), scales=zs[:], in_=z[:])
+            res = bank(4 + c, "res%d" % c)
+            nc.tensor.matmul_mx(
+                out=res[:, :CHUNK],
+                lhsT=w2w[:].bitcast(FP4X4),
+                lhsT_scale=w2s[:],
+                rhs=zc[:].bitcast(FP8X4),
+                rhs_scale=zs[:],
+                start=True,
+                stop=True,
+            )
+            o = sb.tile([P, CHUNK], F32, name="o%d" % c)
+            nc.scalar.copy(o[:], res[:, :CHUNK])
+            nc.sync.dma_start(out[:, CHUNK * c : CHUNK * (c + 1)], o[:])

@@ -19,8 +19,6 @@ GELU = mybir.ActivationFunctionType.Gelu_apprx_tanh
 P = 128
 PASSES = K // 512
 HALF = S // 2
-CHUNK = 256
-CHUNKS = U // CHUNK
 
 
 def tile_picked_unet_gelu_p_kernel(
@@ -35,197 +33,260 @@ def tile_picked_unet_gelu_p_kernel(
         def bank(b, name):
             return ps.tile([P, 512], F32, name=name, tag="bank%d" % b)
 
+        def tile(shape, dtype, name, tag=None):
+            return sb.tile(shape, dtype, name=name, tag=tag or name, align_bytes=64)
+
         offs_sb = lists.tile([P, S // 16], U16, name="offs_sb")
         cell_sb = lists.tile([P, S // 16], U16, name="cell_sb")
-        xs = sb.tile([P, T], U8, name="xs", align_bytes=64)
-        nc.vector.memset(xs[:].bitcast(I32), 0)
+        xs = tile([P, T], U8, "xs")
+        nc.gpsimd.memset(xs[:].bitcast(I32), 0)
         nc.sync.dma_start(offs_sb[:], offs)
-        for q in range(4):
-            nc.sync.dma_start(xs[32 * q : 32 * q + 8, :].bitcast(I32), x_scales[:, 4 * q : 4 * q + 4, :].bitcast(I32))
+        nc.sync.dma_start(cell_sb[:], cell)
 
-        w_rows = w1.rearrange("(g k j) (h c) -> h g k j c", g=PASSES, j=4, h=2)
+        w_rows = w1.rearrange("(g k j) c -> g k j c", g=PASSES, j=4)
 
-        def load_w(h, g):
-            raw = sb.tile([P, 4, 256], F32, name="wraw%d%d" % (h, g), tag="wraw%d%d" % (h, g), align_bytes=64)
-            nc.sync.dma_start(raw[:], w_rows[h, g])
+        def load_w(name, g, c0, width):
+            raw = tile([P, 4, width], F32, "%s%d" % (name, g))
+            nc.sync.dma_start(raw[:], w_rows[g][:, :, c0 : c0 + width])
             return raw
 
-        skip_rows = skip.rearrange("(h p u e) v -> h u p e v", h=2, u=2, e=2)
-
-        def load_skip(h, u):
-            sk = sb.tile([P, U], F32, name="skip%d%d" % (h, u))
-            nc.sync.dma_start(sk[:], skip_rows[h, u])
+        def load_skip(w):
+            sk = tile([P, U], F32, "skip%d" % w)
+            if w < 2:
+                rows = skip[P * w : P * (w + 1), :]
+            else:
+                rows = skip[2 * P :, :].rearrange("(r u e) v -> u r e v", u=2, e=2)[w - 2]
+            nc.sync.dma_start(sk[:], rows)
             return sk
 
-        wraw = {}
-        for g in range(PASSES):
-            wraw[0, g] = load_w(0, g)
+        raw0 = [load_w("raw0", g, 0, P) for g in range(PASSES)]
+        for q in range(4):
+            nc.sync.dma_start(xs[32 * q : 32 * q + 8, :].bitcast(I32), x_scales[:, 4 * q : 4 * q + 4, :].bitcast(I32))
         xw = []
         for g in range(PASSES):
-            t = sb.tile([P, T], U32, name="xw%d" % g, align_bytes=64)
+            t = tile([P, T], U32, "xw%d" % g)
             nc.sync.dma_start(t[:].bitcast(I32), x_words[g].rearrange("p n t -> p (n t)").bitcast(I32))
             xw.append(t)
-        nc.sync.dma_start(cell_sb[:], cell)
-        sk = {}
-        sk[0, 0] = load_skip(0, 0)
+        raw1 = [load_w("raw1", g, P, P) for g in range(PASSES)]
+        sk, rawb = [], []
         for g in range(PASSES):
-            wraw[1, g] = load_w(1, g)
-        sk[0, 1] = load_skip(0, 1)
-        sk[1, 0] = load_skip(1, 0)
-        sk[1, 1] = load_skip(1, 1)
-        w2w = sb.tile([P, 2 * N], U8, name="w2w", align_bytes=64)
-        w2s = sb.tile([P, N], U8, name="w2s", align_bytes=64)
+            sk.append(load_skip(g))
+            rawb.append(load_w("rawb", g, 2 * P, 2 * P))
+        for w in (2, 3):
+            sk.append(load_skip(w))
+        w2w = tile([P, 2, 2, 2 * N], U8, "w2w")
+        w2s = tile([P, 2, N], U8, "w2s")
+        nc.vector.memset(w2w[:].bitcast(I32), 0)
         nc.vector.memset(w2s[:].bitcast(I32), 0)
-        nc.sync.dma_start(w2w[:].bitcast(I32), w2_words[0].bitcast(I32))
+        for G in range(2):
+            nc.sync.dma_start(
+                w2w[64 * G : 64 * (G + 1), :, G, :].bitcast(I32),
+                w2_words[0].rearrange("(h r) c -> r h c", h=2).bitcast(I32),
+            )
         for q in range(4):
-            nc.sync.dma_start(w2s[32 * q : 32 * q + 4, :].bitcast(I32), w2_scales[0, 4 * q : 4 * q + 4, :].bitcast(I32))
+            nc.sync.dma_start(
+                w2s[32 * q : 32 * q + 4, :, :].bitcast(I32),
+                w2_scales[0].rearrange("(h q a) c -> q a h c", h=2, q=2)[q % 2].bitcast(I32),
+            )
 
-        ident = sb.tile([P, P], F32, name="ident")
+        ident = tile([P, P], F32, "ident")
         make_identity(nc, ident[:])
         win = {}
-        for h in range(2):
-            for u in range(2):
-                win[h, u] = sb.tile([P, U], F32, name="win%d%d" % (h, u))
-                nc.vector.memset(win[h, u][:], 0.0)
+        for w in range(4):
+            win[w] = tile([P, U], F32, "win%d" % w)
+        nc.vector.memset(win[0][:], 0.0)
+        nc.scalar.activation(win[1][:], win[0][:], GELU)
 
-        wb, wc, ws = {}, {}, {}
-        for h in range(2):
-            for u in range(2):
-                wb[h, u] = sb.tile([P, PASSES * 512], BF16, name="wb%d%d" % (h, u), align_bytes=64)
-                wc[h, u] = sb.tile([P, PASSES * P], U32, name="wc%d%d" % (h, u), align_bytes=64)
-                ws[h, u] = sb.tile([P, PASSES * P], U8, name="ws%d%d" % (h, u), align_bytes=64)
+        wb = [tile([P, PASSES * 512], BF16, "wb0"), tile([P, PASSES * 512], BF16, "wb1"), tile([P, 4 * 512], BF16, "wbb")]
+        wc = [tile([P, PASSES * P], U32, "wc%d" % w) for w in range(4)]
+        ws = [tile([P, PASSES * P], U8, "ws%d" % w) for w in range(4)]
 
-        def cast_w(copy, h, g, u):
-            src = wraw[h, g][:].rearrange("k j (q u e) -> k u q j e", u=2, e=2)[:, u]
-            dst = wb[h, u][:, 512 * g : 512 * (g + 1)].rearrange("k (q e j) -> k q j e", e=2, j=4)
-            copy(dst, src)
+        def cast_a(copy, w, raw, g):
+            copy(
+                wb[w][:, 512 * g : 512 * (g + 1)].rearrange("k (c i j) -> k c j i", i=4, j=4),
+                raw[g][:].rearrange("k j (c i) -> k c j i", i=4),
+            )
 
-        def quant_w(h, u):
-            nc.vector.quantize_mx(out=wc[h, u][:].bitcast(FP8X4), scales=ws[h, u][:], in_=wb[h, u][:])
+        def cast_b(g):
+            nc.scalar.copy(
+                wb[2][:].rearrange("k (u g r e j) -> k g r j u e", u=2, g=PASSES, e=2, j=4)[:, g],
+                rawb[g][:].rearrange("k j (r u e) -> k r j u e", u=2, e=2),
+            )
+
+        def quant_w(w, src):
+            nc.vector.quantize_mx(out=wc[w][:].bitcast(FP8X4), scales=ws[w][:], in_=src)
 
         for g in range(PASSES):
-            for u in range(2):
-                cast_w(nc.vector.tensor_copy, 0, g, u)
-        for u in range(2):
-            quant_w(0, u)
+            cast_a(nc.scalar.copy, 0, raw0, g)
+        quant_w(0, wb[0][:])
+        for w in (2, 3):
+            nc.scalar.copy(win[w][:], win[0][:])
 
-        xsg = sb.tile([P, S], U8, name="xsg", align_bytes=64)
+        xsg = tile([P, S], U8, "xsg")
         nc.vector.tensor_copy(xsg[:], xs[:].indirect(offs_sb[:]))
-        xg = [sb.tile([P, S], U32, name="xg%d" % g, align_bytes=64) for g in range(PASSES)]
+        xg = [tile([P, S], U32, "xg%d" % g) for g in range(PASSES)]
         nc.vector.tensor_copy(xg[0][:], xw[0][:].indirect(offs_sb[:]))
         for a in range(2):
             nc.vector.tensor_copy(xg[1][:, HALF * a : HALF * (a + 1)], xw[1][:].indirect(offs_sb[:, 16 * a : 16 * (a + 1)]))
 
-        def first_product(acc, h, u, g, cols):
-            nc.tensor.matmul_mx(
-                out=acc,
-                lhsT=wc[h, u][:, P * g : P * (g + 1)].bitcast(FP8X4),
-                lhsT_scale=ws[h, u][:, P * g : P * (g + 1)],
-                rhs=xg[g][:, cols].bitcast(FP8X4),
-                rhs_scale=xsg[4 * g : P, cols],
-                start=(g == 0),
-                stop=(g == PASSES - 1),
-            )
-
-        acc = {}
-        for a in range(2):
-            for u in range(2):
-                acc[a, u] = bank(6 * a + u, "acc%d%d" % (a, u))
-        for g in range(PASSES):
-            for a in range(2):
-                for u in range(2):
-                    first_product(acc[a, u][:, :HALF], 0, u, g, slice(HALF * a, HALF * (a + 1)))
-
-        ha = sb.tile([P, 2, HALF], F32, name="ha")
-        for u in range(2):
-            nc.scalar.activation(ha[:, u, :], acc[0, u][:, :HALF], GELU)
-        for u in range(2):
-            nc.vector.tensor_copy(win[0, u][:].indirect(cell_sb[:, 0:16]), ha[:, u, :])
-
-        for g in range(PASSES):
-            for u in range(2):
-                cast_w(nc.scalar.copy, 1, g, u)
-        for u in range(2):
-            quant_w(1, u)
-
-        hb = sb.tile([P, 2, HALF], F32, name="hb", tag="wraw11", align_bytes=64)
-        for u in range(2):
-            nc.scalar.activation(hb[:, u, :], acc[1, u][:, :HALF], GELU)
-        for u in range(2):
-            nc.vector.tensor_copy(win[0, u][:].indirect(cell_sb[:, 16:32]), hb[:, u, :])
-
-        hfull = {}
-        for u in range(2):
-            accb = bank(u, "accb%d" % u)
+        def first_product(acc, w, cols):
             for g in range(PASSES):
-                first_product(accb[:], 1, u, g, slice(0, S))
-            hfull[u] = sb.tile([P, S], F32, name="hfull%d" % u)
-            nc.scalar.activation(hfull[u][:], accb[:], GELU)
+                nc.tensor.matmul_mx(
+                    out=acc,
+                    lhsT=wc[w][:, P * g : P * (g + 1)].bitcast(FP8X4),
+                    lhsT_scale=ws[w][:, P * g : P * (g + 1)],
+                    rhs=xg[g][:, cols].bitcast(FP8X4),
+                    rhs_scale=xsg[4 * g : P, cols],
+                    start=(g == 0),
+                    stop=(g == PASSES - 1),
+                )
 
-        zt = {}
-        for u in range(2):
-            for c in range(CHUNKS):
-                zt[u, c] = sb.tile([P, 2, 256], BF16, name="zt%d%d" % (u, c), align_bytes=64)
+        hs = {}
 
-        def turn_sum(h, u, banks, copies):
-            per_bank = 8 // len(banks)
-            tiles = [bank(b, "zT%d%d%d" % (h, u, b)) for b in banks]
-            for src, first in ((sk[h, u], True), (win[h, u], False)):
-                for vt in range(8):
-                    s = vt % per_bank
+        def gelu_scatter(w, a, acc, tag=None):
+            h = tile([P, HALF], F32, "h%d%d" % (w, a), tag)
+            nc.scalar.activation(h[:], acc, GELU)
+            hs[w, a] = h
+            nc.vector.tensor_copy(win[w][:].indirect(cell_sb[:, 16 * a : 16 * (a + 1)]), h[:])
+
+        def turn(tiles, src, first):
+            vt = 0
+            for t, count in tiles:
+                for s in range(count):
                     nc.tensor.matmul(
-                        tiles[vt // per_bank][:, P * s : P * (s + 1)],
+                        t[:, P * s : P * (s + 1)],
                         src[:, P * vt : P * (vt + 1)],
                         ident[:],
                         is_transpose=True,
                         start=(first and s == 0),
-                        stop=(not first and s == per_bank - 1),
+                        stop=(not first and s == count - 1),
                     )
-            for c in range(CHUNKS):
-                s = (2 * c) % per_bank
-                src = tiles[2 * c // per_bank][:, P * s : P * (s + 2)].rearrange("v (s q) -> v s q", s=2)
-                copies[c](zt[u, c][:, :, P * h : P * (h + 1)], src)
+                    vt += 1
 
-        on_scalar = [nc.scalar.copy] * CHUNKS
-        in_turn = [nc.scalar.copy, nc.vector.tensor_copy] * (CHUNKS // 2)
+        def turn_sum(w, banks, counts=(4, 4)):
+            tiles = [(bank(b, "zT%d%d" % (w, b)), n) for b, n in zip(banks, counts)]
+            turn(tiles, sk[w], True)
+            turn(tiles, win[w], False)
+            return [t for t, n in tiles]
 
-        turn_sum(0, 0, (2, 3), on_scalar)
-        turn_sum(0, 1, (4, 5), on_scalar)
-        nc.vector.tensor_copy(win[1, 0][:].indirect(cell_sb[:]), hfull[0][:])
-        nc.vector.tensor_copy(win[1, 1][:].indirect(cell_sb[:]), hfull[1][:])
-        turn_sum(1, 0, (2, 3), on_scalar)
+        acc0 = [bank(a, "acc0%d" % a) for a in range(2)]
+        for a in range(2):
+            first_product(acc0[a][:, :HALF], 0, slice(HALF * a, HALF * (a + 1)))
+        gelu_scatter(0, 0, acc0[0][:, :HALF])
+        for g in range(PASSES):
+            cast_a(nc.scalar.copy, 1, raw1, g)
+        quant_w(1, wb[1][:])
+        gelu_scatter(0, 1, acc0[1][:, :HALF], "raw11")
 
-        back = [bank(c, "back%d" % c) for c in range(CHUNKS)]
+        acc1 = [bank(a, "acc1%d" % a) for a in range(2)]
+        for a in range(2):
+            first_product(acc1[a][:, :HALF], 1, slice(HALF * a, HALF * (a + 1)))
+        gelu_scatter(1, 0, acc1[0][:, :HALF])
+        for g in range(PASSES):
+            cast_b(g)
+        for u in range(2):
+            quant_w(2 + u, wb[2][:, 1024 * u : 1024 * (u + 1)])
+        gelu_scatter(1, 1, acc1[1][:, :HALF], "rawb1")
 
-        def turn_back(u, c):
+        acc2 = bank(0, "acc2")
+        first_product(acc2[:], 2, slice(0, S))
+        acc3 = bank(1, "acc3")
+        first_product(acc3[:], 3, slice(0, S))
+        h2 = tile([P, S], F32, "h2")
+        nc.scalar.activation(h2[:], acc2[:], GELU)
+        nc.vector.tensor_copy(win[2][:].indirect(cell_sb[:]), h2[:])
+
+        zt_a = tile([P, 2, 2, 2, 2, P], BF16, "zta", "wbb")
+        zta = [zt_a[:, c] for c in range(2)]
+
+        def round_a(w, tiles, c):
             for s in range(2):
-                nc.tensor.transpose(
-                    back[c][:, CHUNK * u + P * s : CHUNK * u + P * (s + 1)], zt[u, c][:, s, :].bitcast(F32), ident[:]
+                nc.scalar.copy(
+                    zta[c][:, s, :, :, 64 * w : 64 * (w + 1)].rearrange("v u g (r e) -> v u g r e", e=2),
+                    tiles[c][:, 256 * s : 256 * (s + 1)].rearrange("v (g r u e) -> v u g r e", g=2, u=2, e=2),
                 )
 
-        for c in range(CHUNKS):
-            turn_back(0, c)
-        turn_sum(1, 1, (4, 5, 6, 7), in_turn)
-        for c in range(CHUNKS):
-            turn_back(1, c)
-        for c in range(CHUNKS):
-            z = sb.tile([P, 4 * CHUNK], BF16, name="z%d" % c, align_bytes=64)
-            in_turn[c](
-                z[:].bitcast(F32).rearrange("p (v u) -> p v u", u=2), back[c][:].rearrange("p (u v) -> p v u", u=2)
+        t0 = turn_sum(0, (2, 3))
+        for c in range(2):
+            round_a(0, t0, c)
+        t1 = turn_sum(1, (4, 5))
+        round_a(1, t1, 0)
+        late = tile([P, S], F32, "late")
+        nc.scalar.activation(late[:], acc3[:], GELU)
+        nc.vector.tensor_copy(win[3][:].indirect(cell_sb[:]), late[:])
+        round_a(1, t1, 1)
+
+        def turn_back(back, src, s, u, pairs):
+            at = P * (pairs * u + s)
+            nc.tensor.transpose(back[:, at : at + P], src.bitcast(F32), ident[:])
+
+        def weave(copy, back, name, pairs):
+            z = tile([P, 512 * pairs], BF16, name)
+            copy(
+                z[:].bitcast(F32).rearrange("p (v u) -> p v u", u=2),
+                back[:, : 256 * pairs].rearrange("p (u v) -> p v u", u=2),
             )
-            zc = sb.tile([P, CHUNK], U32, name="zc%d" % c, align_bytes=64)
-            zs = sb.tile([P, CHUNK], U8, name="zs%d" % c, align_bytes=64)
+            return z
+
+        za = []
+        for c in range(2):
+            back = bank(2 + c, "backa%d" % c)
+            for s in range(2):
+                for u in range(2):
+                    turn_back(back, zta[c][:, s, u].rearrange("v g m -> v (g m)"), s, u, 2)
+            za.append(weave(nc.scalar.copy, back, "za%d" % c, 2))
+
+        def round_b(copy, src, pairs, name):
+            zt = tile([P, 256 * pairs], BF16, name)
+            copy(zt[:], src[:, : 256 * pairs])
+            return zt
+
+        chunks = ((0, 2), (2, 1), (3, 1))
+        t2 = turn_sum(2, (6, 7))
+        zt2 = [round_b(nc.scalar.copy, t2[c], 2, "zt2%d" % c) for c in range(2)]
+        backb = [bank(b, "backb%d" % b) for b in (6, 7, 3)]
+        for i, (j0, pairs) in enumerate(chunks):
+            for s in range(pairs):
+                j = j0 + s
+                turn_back(backb[i], zt2[j // 2][:, 256 * (j % 2) : 256 * (j % 2 + 1)], s, 0, pairs)
+        t3 = turn_sum(3, (4, 5, 2), (4, 2, 2))
+
+        def quant_z(z, name, pairs):
+            zc = tile([P, P * pairs], U32, "c" + name)
+            zs = tile([P, P * pairs], U8, "s" + name)
             nc.vector.quantize_mx(out=zc[:].bitcast(FP8X4), scales=zs[:], in_=z[:])
-            res = bank(4 + c, "res%d" % c)
-            nc.tensor.matmul_mx(
-                out=res[:, :CHUNK],
-                lhsT=w2w[:].bitcast(FP4X4),
-                lhsT_scale=w2s[:],
-                rhs=zc[:].bitcast(FP8X4),
-                rhs_scale=zs[:],
-                start=True,
-                stop=True,
-            )
-            o = sb.tile([P, CHUNK], F32, name="o%d" % c)
-            nc.scalar.copy(o[:], res[:, :CHUNK])
-            nc.sync.dma_start(out[:, CHUNK * c : CHUNK * (c + 1)], o[:])
+            return zc, zs
+
+        def second_product(res, h, zc, zs, s_from, s_to, first, last):
+            for G in range(2):
+                at = 256 * s_to + P * G
+                nc.tensor.matmul_mx(
+                    out=res[:, at : at + P],
+                    lhsT=w2w[:, h, G, :].bitcast(FP4X4),
+                    lhsT_scale=w2s[:, h, :],
+                    rhs=zc[:, P * s_from : P * (s_from + 1)].bitcast(FP8X4),
+                    rhs_scale=zs[:, P * s_from : P * (s_from + 1)],
+                    start=(first and G == 0),
+                    stop=(last and G == 1),
+                )
+
+        sc, ve = nc.scalar.copy, nc.vector.tensor_copy
+        qa = [quant_z(za[c], "za%d" % c, 2) for c in range(2)]
+        for i, (j0, pairs) in enumerate(chunks):
+            zt = round_b((sc, ve, sc)[i], t3[i], pairs, "zt3%d" % i)
+            for s in range(pairs):
+                turn_back(backb[i], zt[:, 256 * s : 256 * (s + 1)], s, 1, pairs)
+        zb = [weave((ve, sc, sc)[i], backb[i], "zb%d" % i, pairs) for i, (j0, pairs) in enumerate(chunks)]
+        res = [bank(b, "res%d" % b) for b in (0, 1, 4)]
+        for i, (j0, pairs) in enumerate(chunks):
+            for s in range(pairs):
+                j = j0 + s
+                second_product(res[i], 0, qa[j // 2][0], qa[j // 2][1], j % 2, s, s == 0, False)
+        for i, (j0, pairs) in enumerate(chunks):
+            zc, zs = quant_z(zb[i], "zb%d" % i, pairs)
+            for s in range(pairs):
+                second_product(res[i], 1, zc, zs, s, s, False, s == pairs - 1)
+        for i, (j0, pairs) in enumerate(chunks):
+            o = tile([P, 256 * pairs], F32, "o%d" % i)
+            (sc, ve, sc)[i](o[:], res[i][:, : 256 * pairs])
+            nc.sync.dma_start(out[:, 256 * j0 : 256 * (j0 + pairs)], o[:])

@@ -70,8 +70,8 @@ def tile_picked_unet_gelu_p_kernel(
         raw1 = [load_w("raw1", g, P, P) for g in range(PASSES)]
         sk, rawb = [], []
         for g in range(PASSES):
-            sk.append(load_skip(g))
             rawb.append(load_w("rawb", g, 2 * P, 2 * P))
+            sk.append(load_skip(g))
         for w in (2, 3):
             sk.append(load_skip(w))
         w2w = tile([P, 2, 2, 2 * N], U8, "w2w")

@@ -41,7 +41,6 @@ def tile_picked_unet_gelu_p_kernel(
         xs = tile([P, T], U8, "xs")
         nc.gpsimd.memset(xs[:].bitcast(I32), 0)
         nc.sync.dma_start(offs_sb[:], offs)
-        nc.sync.dma_start(cell_sb[:], cell)
 
         w_rows = w1.rearrange("(g k j) c -> g k j c", g=PASSES, j=4)
 
@@ -60,13 +59,15 @@ def tile_picked_unet_gelu_p_kernel(
             return sk
 
         raw0 = [load_w("raw0", g, 0, P) for g in range(PASSES)]
-        for q in range(4):
-            nc.sync.dma_start(xs[32 * q : 32 * q + 8, :].bitcast(I32), x_scales[:, 4 * q : 4 * q + 4, :].bitcast(I32))
         xw = []
         for g in range(PASSES):
+            for q in range(4):
+                at = 32 * q + 4 * g
+                nc.sync.dma_start(xs[at : at + 4, :].bitcast(I32), x_scales[g, 4 * q : 4 * q + 4, :].bitcast(I32))
             t = tile([P, T], U32, "xw%d" % g)
             nc.sync.dma_start(t[:].bitcast(I32), x_words[g].rearrange("p n t -> p (n t)").bitcast(I32))
             xw.append(t)
+        nc.sync.dma_start(cell_sb[:], cell)
         raw1 = [load_w("raw1", g, P, P) for g in range(PASSES)]
         sk, rawb = [], []
         for g in range(PASSES):
@@ -288,5 +289,5 @@ def tile_picked_unet_gelu_p_kernel(
                 second_product(res[i], 1, zc, zs, s, s, False, s == pairs - 1)
         for i, (j0, pairs) in enumerate(chunks):
             o = tile([P, 256 * pairs], F32, "o%d" % i)
-            (sc, ve, sc)[i](o[:], res[i][:, : 256 * pairs])
+            (sc, ve, ve)[i](o[:], res[i][:, : 256 * pairs])
             nc.sync.dma_start(out[:, 256 * j0 : 256 * (j0 + pairs)], o[:])

@@ -40,7 +40,6 @@ def tile_picked_unet_gelu_p_kernel(
         cell_sb = lists.tile([P, S // 16], U16, name="cell_sb")
         xs = tile([P, T], U8, "xs")
         nc.gpsimd.memset(xs[:].bitcast(I32), 0)
-        nc.sync.dma_start(offs_sb[:], offs)
 
         w_rows = w1.rearrange("(g k j) c -> g k j c", g=PASSES, j=4)
 
@@ -58,15 +57,23 @@ def tile_picked_unet_gelu_p_kernel(
             nc.sync.dma_start(sk[:], rows)
             return sk
 
-        raw0 = [load_w("raw0", g, 0, P) for g in range(PASSES)]
-        xw = []
-        for g in range(PASSES):
+        xw = [tile([P, T], U32, "xw%d" % g) for g in range(PASSES)]
+
+        def load_x(g, lo, hi):
+            nc.sync.dma_start(
+                xw[g][:, lo:hi].bitcast(I32), x_words[g].rearrange("p n t -> p (n t)").bitcast(I32)[:, lo:hi]
+            )
+
+        def load_scales(g):
             for q in range(4):
                 at = 32 * q + 4 * g
                 nc.sync.dma_start(xs[at : at + 4, :].bitcast(I32), x_scales[g, 4 * q : 4 * q + 4, :].bitcast(I32))
-            t = tile([P, T], U32, "xw%d" % g)
-            nc.sync.dma_start(t[:].bitcast(I32), x_words[g].rearrange("p n t -> p (n t)").bitcast(I32))
-            xw.append(t)
+
+        raw0 = [load_w("raw0", g, 0, P) for g in range(PASSES)]
+        nc.sync.dma_start(offs_sb[:], offs)
+        for g in range(PASSES):
+            load_scales(g)
+            load_x(g, 0, T)
         nc.sync.dma_start(cell_sb[:], cell)
         raw1 = [load_w("raw1", g, P, P) for g in range(PASSES)]
         sk, rawb = [], []
@@ -97,8 +104,10 @@ def tile_picked_unet_gelu_p_kernel(
             win[w] = tile([P, U], F32, "win%d" % w)
         nc.vector.memset(win[0][:], 0.0)
         nc.scalar.activation(win[1][:], win[0][:], GELU)
+        for w in (2, 3):
+            nc.vector.memset(win[w][:], 0.0)
 
-        wb = [tile([P, PASSES * 512], BF16, "wb0"), tile([P, PASSES * 512], BF16, "wb1"), tile([P, 4 * 512], BF16, "wbb")]
+        wb = [tile([P, PASSES * 512], BF16, "wb%d" % w) for w in range(4)]
         wc = [tile([P, PASSES * P], U32, "wc%d" % w) for w in range(4)]
         ws = [tile([P, PASSES * P], U8, "ws%d" % w) for w in range(4)]
 
@@ -108,10 +117,10 @@ def tile_picked_unet_gelu_p_kernel(
                 raw[g][:].rearrange("k j (c i) -> k c j i", i=4),
             )
 
-        def cast_b(g):
+        def cast_b(g, u):
             nc.scalar.copy(
-                wb[2][:].rearrange("k (u g r e j) -> k g r j u e", u=2, g=PASSES, e=2, j=4)[:, g],
-                rawb[g][:].rearrange("k j (r u e) -> k r j u e", u=2, e=2),
+                wb[2 + u][:].rearrange("k (g r e j) -> k g r j e", g=PASSES, e=2, j=4)[:, g],
+                rawb[g][:].rearrange("k j (r u e) -> k u r j e", u=2, e=2)[:, u],
             )
 
         def quant_w(w, src):
@@ -120,35 +129,38 @@ def tile_picked_unet_gelu_p_kernel(
         for g in range(PASSES):
             cast_a(nc.scalar.copy, 0, raw0, g)
         quant_w(0, wb[0][:])
-        for w in (2, 3):
-            nc.scalar.copy(win[w][:], win[0][:])
 
         xsg = tile([P, S], U8, "xsg")
+        xg0 = tile([P, S], U32, "xg0")
+        xg1 = [tile([P, HALF], U32, "xg1%d" % a) for a in range(2)]
         nc.vector.tensor_copy(xsg[:], xs[:].indirect(offs_sb[:]))
-        xg = [tile([P, S], U32, "xg%d" % g) for g in range(PASSES)]
-        nc.vector.tensor_copy(xg[0][:], xw[0][:].indirect(offs_sb[:]))
+        nc.vector.tensor_copy(xg0[:], xw[0][:].indirect(offs_sb[:]))
         for a in range(2):
-            nc.vector.tensor_copy(xg[1][:, HALF * a : HALF * (a + 1)], xw[1][:].indirect(offs_sb[:, 16 * a : 16 * (a + 1)]))
+            nc.vector.tensor_copy(xg1[a][:], xw[1][:].indirect(offs_sb[:, 16 * a : 16 * (a + 1)]))
 
-        def first_product(acc, w, cols):
-            for g in range(PASSES):
-                nc.tensor.matmul_mx(
-                    out=acc,
-                    lhsT=wc[w][:, P * g : P * (g + 1)].bitcast(FP8X4),
-                    lhsT_scale=ws[w][:, P * g : P * (g + 1)],
-                    rhs=xg[g][:, cols].bitcast(FP8X4),
-                    rhs_scale=xsg[4 * g : P, cols],
-                    start=(g == 0),
-                    stop=(g == PASSES - 1),
-                )
+        def first_product(acc, w, cols, passes=range(PASSES)):
+            lo, hi = cols.start, cols.stop
+            for g in passes:
+                cuts = [(lo, hi)] if g == 0 or hi - lo <= HALF else [(lo, HALF), (HALF, hi)]
+                for a, b in cuts:
+                    words = xg0[:, a:b] if g == 0 else xg1[a // HALF][:, a % HALF : a % HALF + b - a]
+                    nc.tensor.matmul_mx(
+                        out=acc[:, a - lo : b - lo],
+                        lhsT=wc[w][:, P * g : P * (g + 1)].bitcast(FP8X4),
+                        lhsT_scale=ws[w][:, P * g : P * (g + 1)],
+                        rhs=words.bitcast(FP8X4),
+                        rhs_scale=xsg[4 * g : P, a:b],
+                        start=(g == 0),
+                        stop=(g == PASSES - 1 and b == hi),
+                    )
 
         hs = {}
 
-        def gelu_scatter(w, a, acc, tag=None):
-            h = tile([P, HALF], F32, "h%d%d" % (w, a), tag)
+        def gelu_scatter(w, lo, hi, acc, tag=None):
+            h = tile([P, hi - lo], F32, "h%d_%d" % (w, lo), tag)
             nc.scalar.activation(h[:], acc, GELU)
-            hs[w, a] = h
-            nc.vector.tensor_copy(win[w][:].indirect(cell_sb[:, 16 * a : 16 * (a + 1)]), h[:])
+            hs[w, lo] = h
+            nc.vector.tensor_copy(win[w][:].indirect(cell_sb[:, lo // 16 : hi // 16]), h[:])
 
         def turn(tiles, src, first):
             vt = 0
@@ -170,35 +182,33 @@ def tile_picked_unet_gelu_p_kernel(
             turn(tiles, win[w], False)
             return [t for t, n in tiles]
 
-        acc0 = [bank(a, "acc0%d" % a) for a in range(2)]
-        for a in range(2):
-            first_product(acc0[a][:, :HALF], 0, slice(HALF * a, HALF * (a + 1)))
-        gelu_scatter(0, 0, acc0[0][:, :HALF])
+        cuts = ((0, HALF), (HALF, S))
+        acc0 = [bank(b, "acc0%d" % b) for b in (0, 1)]
+        for g in range(PASSES):
+            for a, (lo, hi) in enumerate(cuts):
+                first_product(acc0[a][:, : hi - lo], 0, slice(lo, hi), (g,))
+        gelu_scatter(0, 0, HALF, acc0[0][:, :HALF])
         for g in range(PASSES):
             cast_a(nc.scalar.copy, 1, raw1, g)
         quant_w(1, wb[1][:])
-        gelu_scatter(0, 1, acc0[1][:, :HALF], "raw11")
+        gelu_scatter(0, HALF, S, acc0[1][:, :HALF], "raw11")
 
         acc1 = [bank(a, "acc1%d" % a) for a in range(2)]
         for a in range(2):
             first_product(acc1[a][:, :HALF], 1, slice(HALF * a, HALF * (a + 1)))
-        gelu_scatter(1, 0, acc1[0][:, :HALF])
+        gelu_scatter(1, 0, HALF, acc1[0][:, :HALF])
         for g in range(PASSES):
-            cast_b(g)
+            for u in range(2):
+                cast_b(g, u)
         for u in range(2):
-            quant_w(2 + u, wb[2][:, 1024 * u : 1024 * (u + 1)])
-        gelu_scatter(1, 1, acc1[1][:, :HALF], "rawb1")
+            quant_w(2 + u, wb[2 + u][:])
+        gelu_scatter(1, HALF, S, acc1[1][:, :HALF], "rawb1")
 
         acc2 = bank(0, "acc2")
         first_product(acc2[:], 2, slice(0, S))
-        acc3 = bank(1, "acc3")
-        first_product(acc3[:], 3, slice(0, S))
-        h2 = tile([P, S], F32, "h2")
-        nc.scalar.activation(h2[:], acc2[:], GELU)
-        nc.vector.tensor_copy(win[2][:].indirect(cell_sb[:]), h2[:])
+        gelu_scatter(2, 0, S, acc2[:])
 
-        zt_a = tile([P, 2, 2, 2, 2, P], BF16, "zta", "wbb")
-        zta = [zt_a[:, c] for c in range(2)]
+        zta = [tile([P, 2, 2, 2, P], BF16, "zta%d" % c, ("wb3", "rawb1")[c]) for c in range(2)]
 
         def round_a(w, tiles, c):
             for s in range(2):
@@ -212,57 +222,32 @@ def tile_picked_unet_gelu_p_kernel(
             round_a(0, t0, c)
         t1 = turn_sum(1, (4, 5))
         round_a(1, t1, 0)
-        late = tile([P, S], F32, "late")
-        nc.scalar.activation(late[:], acc3[:], GELU)
-        nc.vector.tensor_copy(win[3][:].indirect(cell_sb[:]), late[:])
+        acc3 = [bank(3 + a, "acc3%d" % a) for a in range(2)]
+        for a in range(2):
+            first_product(acc3[a][:, :HALF], 3, slice(HALF * a, HALF * (a + 1)))
+        gelu_scatter(3, 0, HALF, acc3[0][:, :HALF])
         round_a(1, t1, 1)
 
         def turn_back(back, src, s, u, pairs):
             at = P * (pairs * u + s)
             nc.tensor.transpose(back[:, at : at + P], src.bitcast(F32), ident[:])
 
-        def weave(copy, back, name, pairs):
-            z = tile([P, 512 * pairs], BF16, name)
+        def weave(copy, back, z, pairs):
             copy(
-                z[:].bitcast(F32).rearrange("p (v u) -> p v u", u=2),
+                z.bitcast(F32).rearrange("p (v u) -> p v u", u=2),
                 back[:, : 256 * pairs].rearrange("p (u v) -> p v u", u=2),
             )
-            return z
 
-        za = []
-        for c in range(2):
-            back = bank(2 + c, "backa%d" % c)
-            for s in range(2):
-                for u in range(2):
-                    turn_back(back, zta[c][:, s, u].rearrange("v g m -> v (g m)"), s, u, 2)
-            za.append(weave(nc.scalar.copy, back, "za%d" % c, 2))
-
-        def round_b(copy, src, pairs, name):
-            zt = tile([P, 256 * pairs], BF16, name)
-            copy(zt[:], src[:, : 256 * pairs])
-            return zt
-
-        chunks = ((0, 2), (2, 1), (3, 1))
-        t2 = turn_sum(2, (6, 7))
-        zt2 = [round_b(nc.scalar.copy, t2[c], 2, "zt2%d" % c) for c in range(2)]
-        backb = [bank(b, "backb%d" % b) for b in (6, 7, 3)]
-        for i, (j0, pairs) in enumerate(chunks):
-            for s in range(pairs):
-                j = j0 + s
-                turn_back(backb[i], zt2[j // 2][:, 256 * (j % 2) : 256 * (j % 2 + 1)], s, 0, pairs)
-        t3 = turn_sum(3, (4, 5, 2), (4, 2, 2))
-
-        def quant_z(z, name, pairs):
-            zc = tile([P, P * pairs], U32, "c" + name)
-            zs = tile([P, P * pairs], U8, "s" + name)
-            nc.vector.quantize_mx(out=zc[:].bitcast(FP8X4), scales=zs[:], in_=z[:])
+        def quant_z(z, name, words):
+            zc = tile([P, words], U32, "c" + name)
+            zs = tile([P, words], U8, "s" + name)
+            nc.vector.quantize_mx(out=zc[:].bitcast(FP8X4), scales=zs[:], in_=z)
             return zc, zs
 
-        def second_product(res, h, zc, zs, s_from, s_to, first, last):
+        def second_product(res, j, h, zc, zs, s_from, first, last):
             for G in range(2):
-                at = 256 * s_to + P * G
                 nc.tensor.matmul_mx(
-                    out=res[:, at : at + P],
+                    out=res[:, P * G : P * (G + 1)],
                     lhsT=w2w[:, h, G, :].bitcast(FP4X4),
                     lhsT_scale=w2s[:, h, :],
                     rhs=zc[:, P * s_from : P * (s_from + 1)].bitcast(FP8X4),
@@ -271,23 +256,57 @@ def tile_picked_unet_gelu_p_kernel(
                     stop=(last and G == 1),
                 )
 
+        za = [tile([P, 1024], BF16, "za%d" % c) for c in range(2)]
+
+        def finish_a(c):
+            back = bank(2 + c, "backa%d" % c)
+            for s in range(2):
+                for u in range(2):
+                    turn_back(back, zta[c][:, s, u].rearrange("v g m -> v (g m)"), s, u, 2)
+            weave(nc.scalar.copy, back, za[c][:], 2)
+
+        finish_a(0)
+        qa = [quant_z(za[0][:], "za0", 256)]
+        gelu_scatter(3, HALF, S, acc3[1][:, :HALF], "wb3")
+        finish_a(1)
+
+        def round_b(copy, src, pairs, name):
+            zt = tile([P, 256 * pairs], BF16, name)
+            copy(zt[:], src[:, : 256 * pairs])
+            return zt
+
+        t2 = turn_sum(2, (5, 4))
+        zt2 = [round_b(nc.scalar.copy, t2[c], 2, "zt2%d" % c) for c in range(2)]
+        def pairs_of_window_2(j):
+            return zt2[j // 2][:, 256 * (j % 2) : 256 * (j % 2 + 1)]
+
+        backb = [bank(2 + j, "backb%d" % j) for j in range(2)]
+        for j in range(2):
+            turn_back(backb[j], pairs_of_window_2(j), 0, 0, 1)
+        res = [bank(b, "res%d" % b) for b in (1, 7)]
+        for j in range(2):
+            second_product(res[j], j, 0, qa[0][0], qa[0][1], j, True, False)
+        t3_banks = (0, 6, 5, 4)
+        t3 = turn_sum(3, t3_banks, (2, 2, 2, 2))
+
         sc, ve = nc.scalar.copy, nc.vector.tensor_copy
-        qa = [quant_z(za[c], "za%d" % c, 2) for c in range(2)]
-        for i, (j0, pairs) in enumerate(chunks):
-            zt = round_b((sc, ve, sc)[i], t3[i], pairs, "zt3%d" % i)
-            for s in range(pairs):
-                turn_back(backb[i], zt[:, 256 * s : 256 * (s + 1)], s, 1, pairs)
-        zb = [weave((ve, sc, sc)[i], backb[i], "zb%d" % i, pairs) for i, (j0, pairs) in enumerate(chunks)]
-        res = [bank(b, "res%d" % b) for b in (0, 1, 4)]
-        for i, (j0, pairs) in enumerate(chunks):
-            for s in range(pairs):
-                j = j0 + s
-                second_product(res[i], 0, qa[j // 2][0], qa[j // 2][1], j % 2, s, s == 0, False)
-        for i, (j0, pairs) in enumerate(chunks):
-            zc, zs = quant_z(zb[i], "zb%d" % i, pairs)
-            for s in range(pairs):
-                second_product(res[i], 1, zc, zs, s, s, False, s == pairs - 1)
-        for i, (j0, pairs) in enumerate(chunks):
-            o = tile([P, 256 * pairs], F32, "o%d" % i)
-            (sc, ve, ve)[i](o[:], res[i][:, : 256 * pairs])
-            nc.sync.dma_start(out[:, 256 * j0 : 256 * (j0 + pairs)], o[:])
+        qa.append(quant_z(za[1][:], "za1", 256))
+        for j in range(4):
+            zt = round_b((sc, ve, sc, ve)[j], t3[j], 1, "zt3%d" % j)
+            if j >= 2:
+                backb.append(bank(t3_banks[j], "backb%d" % j))
+                turn_back(backb[j], pairs_of_window_2(j), 0, 0, 1)
+            turn_back(backb[j], zt[:], 0, 1, 1)
+        zb = [tile([P, 512], BF16, "zb%d" % j) for j in range(4)]
+        for j in range(4):
+            weave((sc, ve, sc, sc)[j], backb[j], zb[j][:], 1)
+        for j in (2, 3):
+            res.append(bank(t3_banks[j - 2], "res%d" % j))
+            second_product(res[j], j, 0, qa[1][0], qa[1][1], j - 2, True, False)
+        for j in range(4):
+            zc, zs = quant_z(zb[j][:], "zb%d" % j, P)
+            second_product(res[j], j, 1, zc, zs, 0, False, True)
+        for j in range(4):
+            o = tile([P, 256], F32, "o%d" % j)
+            (sc, sc, sc, ve)[j](o[:], res[j][:, :256])
+            nc.sync.dma_start(out[:, 256 * j : 256 * (j + 1)], o[:])

@@ -156,6 +156,20 @@ def tile_picked_unet_gelu_p_kernel(
 
         hs = {}
 
+        def sliced_window(w, lo, widths, banks):
+            total = sum(widths)
+            h = tile([P, total], F32, "h%d_%d" % (w, lo))
+            hs[w, lo] = h
+            accs, at = [], lo
+            for width, b in zip(widths, banks):
+                acc = bank(b, "acc%d_%d" % (w, at))
+                first_product(acc[:, :width], w, slice(at, at + width))
+                accs.append((acc, at - lo, width))
+                at = at + width
+            for acc, at, width in accs:
+                nc.scalar.activation(h[:, at : at + width], acc[:, :width], GELU)
+            nc.vector.tensor_copy(win[w][:].indirect(cell_sb[:, lo // 16 : (lo + total) // 16]), h[:])
+
         def gelu_scatter(w, lo, hi, acc, tag=None):
             h = tile([P, hi - lo], F32, "h%d_%d" % (w, lo), tag)
             nc.scalar.activation(h[:], acc, GELU)
@@ -182,31 +196,32 @@ def tile_picked_unet_gelu_p_kernel(
             turn(tiles, win[w], False)
             return [t for t, n in tiles]
 
-        cuts = ((0, HALF), (HALF, S))
-        acc0 = [bank(b, "acc0%d" % b) for b in (0, 1)]
+        cuts = ((0, P), (P, HALF), (HALF, S))
+        acc0 = [bank(b, "acc0%d" % b) for b in (6, 0, 1)]
         for g in range(PASSES):
             for a, (lo, hi) in enumerate(cuts):
                 first_product(acc0[a][:, : hi - lo], 0, slice(lo, hi), (g,))
-        gelu_scatter(0, 0, HALF, acc0[0][:, :HALF])
+        h = tile([P, HALF], F32, "h0_0")
+        hs[0, 0] = h
+        for a in range(2):
+            nc.scalar.activation(h[:, P * a : P * (a + 1)], acc0[a][:, :P], GELU)
+        nc.vector.tensor_copy(win[0][:].indirect(cell_sb[:, : HALF // 16]), h[:])
         for g in range(PASSES):
             cast_a(nc.scalar.copy, 1, raw1, g)
         quant_w(1, wb[1][:])
-        gelu_scatter(0, HALF, S, acc0[1][:, :HALF], "raw11")
+        gelu_scatter(0, HALF, S, acc0[2][:, :HALF], "raw11")
 
-        acc1 = [bank(a, "acc1%d" % a) for a in range(2)]
-        for a in range(2):
-            first_product(acc1[a][:, :HALF], 1, slice(HALF * a, HALF * (a + 1)))
-        gelu_scatter(1, 0, HALF, acc1[0][:, :HALF])
+        sliced_window(1, 0, (P, P), (6, 0))
+        acc1 = bank(1, "acc1")
+        first_product(acc1[:, :HALF], 1, slice(HALF, S))
         for g in range(PASSES):
             for u in range(2):
                 cast_b(g, u)
         for u in range(2):
             quant_w(2 + u, wb[2 + u][:])
-        gelu_scatter(1, HALF, S, acc1[1][:, :HALF], "rawb1")
+        gelu_scatter(1, HALF, S, acc1[:, :HALF], "rawb1")
 
-        acc2 = bank(0, "acc2")
-        first_product(acc2[:], 2, slice(0, S))
-        gelu_scatter(2, 0, S, acc2[:])
+        sliced_window(2, 0, (HALF, P, P), (0, 6, 7))
 
         zta = [tile([P, 2, 2, 2, P], BF16, "zta%d" % c, ("wb3", "rawb1")[c]) for c in range(2)]
 
@@ -286,27 +301,33 @@ def tile_picked_unet_gelu_p_kernel(
         res = [bank(b, "res%d" % b) for b in (1, 7)]
         for j in range(2):
             second_product(res[j], j, 0, qa[0][0], qa[0][1], j, True, False)
-        t3_banks = (0, 6, 5, 4)
-        t3 = turn_sum(3, t3_banks, (2, 2, 2, 2))
+        order = (2, 3, 0, 1)
+        t3_bank = {2: 0, 3: 6, 0: 5, 1: 4}
+        t3 = {j: bank(t3_bank[j], "zT3%d" % j) for j in order}
+        for src, first in ((sk[3], True), (win[3], False)):
+            for j in order:
+                turn([(t3[j], 2)], src[:, 256 * j : 256 * (j + 1)], first)
 
         sc, ve = nc.scalar.copy, nc.vector.tensor_copy
         qa.append(quant_z(za[1][:], "za1", 256))
-        for j in range(4):
-            zt = round_b((sc, ve, sc, ve)[j], t3[j], 1, "zt3%d" % j)
+        backb = {j: backb[j] for j in range(2)}
+        res = {j: res[j] for j in range(2)}
+        for i, j in enumerate(order):
+            zt = round_b((sc, ve, sc, ve)[i], t3[j], 1, "zt3%d" % j)
             if j >= 2:
-                backb.append(bank(t3_banks[j], "backb%d" % j))
+                backb[j] = bank(t3_bank[j], "backb%d" % j)
                 turn_back(backb[j], pairs_of_window_2(j), 0, 0, 1)
             turn_back(backb[j], zt[:], 0, 1, 1)
-        zb = [tile([P, 512], BF16, "zb%d" % j) for j in range(4)]
-        for j in range(4):
-            weave((sc, ve, sc, sc)[j], backb[j], zb[j][:], 1)
+        zb = {j: tile([P, 512], BF16, "zb%d" % j) for j in order}
+        for i, j in enumerate(order):
+            weave((sc, ve, sc, sc)[i], backb[j], zb[j][:], 1)
         for j in (2, 3):
-            res.append(bank(t3_banks[j - 2], "res%d" % j))
+            res[j] = bank(t3_bank[j - 2], "res%d" % j)
             second_product(res[j], j, 0, qa[1][0], qa[1][1], j - 2, True, False)
-        for j in range(4):
+        for j in order:
             zc, zs = quant_z(zb[j][:], "zb%d" % j, P)
             second_product(res[j], j, 1, zc, zs, 0, False, True)
-        for j in range(4):
+        for i, j in enumerate(order):
             o = tile([P, 256], F32, "o%d" % j)
-            (sc, sc, sc, ve)[j](o[:], res[j][:, :256])
+            (sc, ve, sc, ve)[i](o[:], res[j][:, :256])
             nc.sync.dma_start(out[:, 256 * j : 256 * (j + 1)], o[:])

@@ -196,22 +196,15 @@ def tile_picked_unet_gelu_p_kernel(
             turn(tiles, win[w], False)
             return [t for t, n in tiles]
 
-        cuts = ((0, P), (P, HALF), (HALF, S))
-        acc0 = [bank(b, "acc0%d" % b) for b in (6, 0, 1)]
-        for g in range(PASSES):
-            for a, (lo, hi) in enumerate(cuts):
-                first_product(acc0[a][:, : hi - lo], 0, slice(lo, hi), (g,))
-        h = tile([P, HALF], F32, "h0_0")
-        hs[0, 0] = h
-        for a in range(2):
-            nc.scalar.activation(h[:, P * a : P * (a + 1)], acc0[a][:, :P], GELU)
-        nc.vector.tensor_copy(win[0][:].indirect(cell_sb[:, : HALF // 16]), h[:])
+        sliced_window(0, 0, (P, P), (6, 0))
+        acc0 = bank(6, "acc0")
+        first_product(acc0[:, :HALF], 0, slice(HALF, S))
         for g in range(PASSES):
             cast_a(nc.scalar.copy, 1, raw1, g)
         quant_w(1, wb[1][:])
-        gelu_scatter(0, HALF, S, acc0[2][:, :HALF], "raw11")
+        gelu_scatter(0, HALF, S, acc0[:, :HALF], "raw11")
 
-        sliced_window(1, 0, (P, P), (6, 0))
+        sliced_window(1, 0, (P, P), (7, 0))
         acc1 = bank(1, "acc1")
         first_product(acc1[:, :HALF], 1, slice(HALF, S))
         for g in range(PASSES):

@@ -15,6 +15,7 @@ U8 = mybir.dt.uint8
 FP8X4 = mybir.dt.float8_e4m3fn_x4
 FP4X4 = mybir.dt.float4_e2m1fn_x4
 GELU = mybir.ActivationFunctionType.Gelu_apprx_tanh
+COPY = mybir.ActivationFunctionType.Copy
 
 P = 128
 PASSES = K // 512
@@ -75,13 +76,10 @@ def tile_picked_unet_gelu_p_kernel(
             load_scales(g)
             load_x(g, 0, T)
         nc.sync.dma_start(cell_sb[:], cell)
+        rawb = [load_w("rawb", 0, 2 * P, 2 * P)]
         raw1 = [load_w("raw1", g, P, P) for g in range(PASSES)]
-        sk, rawb = [], []
-        for g in range(PASSES):
-            rawb.append(load_w("rawb", g, 2 * P, 2 * P))
-            sk.append(load_skip(g))
-        for w in (2, 3):
-            sk.append(load_skip(w))
+        rawb.append(load_w("rawb", 1, 2 * P, 2 * P))
+        sk = [load_skip(w) for w in range(4)]
         w2w = tile([P, 2, 2, 2 * N], U8, "w2w")
         w2s = tile([P, 2, N], U8, "w2s")
         nc.vector.memset(w2w[:].bitcast(I32), 0)
@@ -99,36 +97,42 @@ def tile_picked_unet_gelu_p_kernel(
 
         ident = tile([P, P], F32, "ident")
         make_identity(nc, ident[:])
-        win = {}
-        for w in range(4):
-            win[w] = tile([P, U], F32, "win%d" % w)
+        win = [tile([P, U], F32, "win%d" % w) for w in range(4)]
         nc.vector.memset(win[0][:], 0.0)
         nc.scalar.activation(win[1][:], win[0][:], GELU)
         for w in (2, 3):
             nc.vector.memset(win[w][:], 0.0)
 
-        wb = [tile([P, PASSES * 512], BF16, "wb%d" % w) for w in range(4)]
-        wc = [tile([P, PASSES * P], U32, "wc%d" % w) for w in range(4)]
-        ws = [tile([P, PASSES * P], U8, "ws%d" % w) for w in range(4)]
+        sc, ve = nc.scalar.copy, nc.vector.tensor_copy
 
-        def cast_a(copy, w, raw, g):
+        def quant(src, name):
+            words = src.shape[1] // 4
+            codes = tile([P, words], U32, "c" + name)
+            scales = tile([P, words], U8, "s" + name)
+            nc.vector.quantize_mx(out=codes[:].bitcast(FP8X4), scales=scales[:], in_=src)
+            return codes, scales
+
+        def cast_a(copy, raw, name):
+            wb = tile([P, 512], BF16, name)
             copy(
-                wb[w][:, 512 * g : 512 * (g + 1)].rearrange("k (c i j) -> k c j i", i=4, j=4),
-                raw[g][:].rearrange("k j (c i) -> k c j i", i=4),
+                wb[:].rearrange("k (c i j) -> k c j i", i=4, j=4),
+                raw[:].rearrange("k j (c i) -> k c j i", i=4),
             )
+            return wb
 
-        def cast_b(g, u):
-            nc.scalar.copy(
-                wb[2 + u][:].rearrange("k (g r e j) -> k g r j e", g=PASSES, e=2, j=4)[:, g],
-                rawb[g][:].rearrange("k j (r u e) -> k u r j e", u=2, e=2)[:, u],
+        def cast_b(copy, raw, name):
+            wb = tile([P, 1024], BF16, name)
+            copy(
+                wb[:].rearrange("k (u r e j) -> k r j u e", u=2, e=2, j=4),
+                raw[:].rearrange("k j (r u e) -> k r j u e", u=2, e=2),
             )
+            return wb
 
-        def quant_w(w, src):
-            nc.vector.quantize_mx(out=wc[w][:].bitcast(FP8X4), scales=ws[w][:], in_=src)
-
+        wq = {}
+        wb0 = [cast_a(sc, raw0[g], "wb0%d" % g) for g in range(PASSES)]
         for g in range(PASSES):
-            cast_a(nc.scalar.copy, 0, raw0, g)
-        quant_w(0, wb[0][:])
+            c, s = quant(wb0[g][:], "w0%d" % g)
+            wq[0, g] = (c[:], s[:])
 
         xsg = tile([P, S], U8, "xsg")
         xg0 = tile([P, S], U32, "xg0")
@@ -138,189 +142,158 @@ def tile_picked_unet_gelu_p_kernel(
         for a in range(2):
             nc.vector.tensor_copy(xg1[a][:], xw[1][:].indirect(offs_sb[:, 16 * a : 16 * (a + 1)]))
 
-        def first_product(acc, w, cols, passes=range(PASSES)):
-            lo, hi = cols.start, cols.stop
-            for g in passes:
-                cuts = [(lo, hi)] if g == 0 or hi - lo <= HALF else [(lo, HALF), (HALF, hi)]
-                for a, b in cuts:
-                    words = xg0[:, a:b] if g == 0 else xg1[a // HALF][:, a % HALF : a % HALF + b - a]
-                    nc.tensor.matmul_mx(
-                        out=acc[:, a - lo : b - lo],
-                        lhsT=wc[w][:, P * g : P * (g + 1)].bitcast(FP8X4),
-                        lhsT_scale=ws[w][:, P * g : P * (g + 1)],
-                        rhs=words.bitcast(FP8X4),
-                        rhs_scale=xsg[4 * g : P, a:b],
-                        start=(g == 0),
-                        stop=(g == PASSES - 1 and b == hi),
-                    )
-
-        hs = {}
-
-        def sliced_window(w, lo, widths, banks):
-            total = sum(widths)
-            h = tile([P, total], F32, "h%d_%d" % (w, lo))
-            hs[w, lo] = h
-            accs, at = [], lo
-            for width, b in zip(widths, banks):
-                acc = bank(b, "acc%d_%d" % (w, at))
-                first_product(acc[:, :width], w, slice(at, at + width))
-                accs.append((acc, at - lo, width))
-                at = at + width
-            for acc, at, width in accs:
-                nc.scalar.activation(h[:, at : at + width], acc[:, :width], GELU)
-            nc.vector.tensor_copy(win[w][:].indirect(cell_sb[:, lo // 16 : (lo + total) // 16]), h[:])
-
-        def gelu_scatter(w, lo, hi, acc, tag=None):
-            h = tile([P, hi - lo], F32, "h%d_%d" % (w, lo), tag)
-            nc.scalar.activation(h[:], acc, GELU)
-            hs[w, lo] = h
-            nc.vector.tensor_copy(win[w][:].indirect(cell_sb[:, lo // 16 : hi // 16]), h[:])
-
-        def turn(tiles, src, first):
-            vt = 0
-            for t, count in tiles:
-                for s in range(count):
-                    nc.tensor.matmul(
-                        t[:, P * s : P * (s + 1)],
-                        src[:, P * vt : P * (vt + 1)],
-                        ident[:],
-                        is_transpose=True,
-                        start=(first and s == 0),
-                        stop=(not first and s == count - 1),
-                    )
-                    vt += 1
-
-        def turn_sum(w, banks, counts=(4, 4)):
-            tiles = [(bank(b, "zT%d%d" % (w, b)), n) for b, n in zip(banks, counts)]
-            turn(tiles, sk[w], True)
-            turn(tiles, win[w], False)
-            return [t for t, n in tiles]
-
-        sliced_window(0, 0, (P, P), (6, 0))
-        acc0 = bank(6, "acc0")
-        first_product(acc0[:, :HALF], 0, slice(HALF, S))
-        for g in range(PASSES):
-            cast_a(nc.scalar.copy, 1, raw1, g)
-        quant_w(1, wb[1][:])
-        gelu_scatter(0, HALF, S, acc0[:, :HALF], "raw11")
-
-        sliced_window(1, 0, (P, P), (7, 0))
-        acc1 = bank(1, "acc1")
-        first_product(acc1[:, :HALF], 1, slice(HALF, S))
-        for g in range(PASSES):
-            for u in range(2):
-                cast_b(g, u)
-        for u in range(2):
-            quant_w(2 + u, wb[2 + u][:])
-        gelu_scatter(1, HALF, S, acc1[:, :HALF], "rawb1")
-
-        sliced_window(2, 0, (HALF, P, P), (0, 6, 7))
-
-        zta = [tile([P, 2, 2, 2, P], BF16, "zta%d" % c, ("wb3", "rawb1")[c]) for c in range(2)]
-
-        def round_a(w, tiles, c):
-            for s in range(2):
-                nc.scalar.copy(
-                    zta[c][:, s, :, :, 64 * w : 64 * (w + 1)].rearrange("v u g (r e) -> v u g r e", e=2),
-                    tiles[c][:, 256 * s : 256 * (s + 1)].rearrange("v (g r u e) -> v u g r e", g=2, u=2, e=2),
+        def first_product(acc, w, lo, hi):
+            for g in range(PASSES):
+                words = xg0[:, lo:hi] if g == 0 else xg1[lo // HALF][:, lo % HALF : lo % HALF + hi - lo]
+                nc.tensor.matmul_mx(
+                    out=acc,
+                    lhsT=wq[w, g][0].bitcast(FP8X4),
+                    lhsT_scale=wq[w, g][1],
+                    rhs=words.bitcast(FP8X4),
+                    rhs_scale=xsg[4 * g : P, lo:hi],
+                    start=(g == 0),
+                    stop=(g == PASSES - 1),
                 )
 
-        t0 = turn_sum(0, (2, 3))
-        for c in range(2):
-            round_a(0, t0, c)
-        t1 = turn_sum(1, (4, 5))
-        round_a(1, t1, 0)
-        acc3 = [bank(3 + a, "acc3%d" % a) for a in range(2)]
-        for a in range(2):
-            first_product(acc3[a][:, :HALF], 3, slice(HALF * a, HALF * (a + 1)))
-        gelu_scatter(3, 0, HALF, acc3[0][:, :HALF])
-        round_a(1, t1, 1)
+        def scatter_s(w, lo, hi, h):
+            nc.scalar.activation(win[w][:].indirect(cell_sb[:, lo // 16 : hi // 16]), h, COPY)
 
-        def turn_back(back, src, s, u, pairs):
-            at = P * (pairs * u + s)
-            nc.tensor.transpose(back[:, at : at + P], src.bitcast(F32), ident[:])
+        def scatter_v(w, lo, hi, h):
+            nc.vector.tensor_copy(win[w][:].indirect(cell_sb[:, lo // 16 : hi // 16]), h)
 
-        def weave(copy, back, z, pairs):
+        def turn(dst, src, start, stop):
+            nc.tensor.matmul(dst, src, ident[:], is_transpose=True, start=start, stop=stop)
+
+        ha = tile([P, 2 * S], F32, "ha")
+        for i, b in enumerate((0, 7)):
+            acc = bank(b, "acc0a%d" % i)
+            first_product(acc[:, :P], 0, P * i, P * (i + 1))
+            nc.scalar.activation(ha[:, P * i : P * (i + 1)], acc[:, :P], GELU)
+        scatter_s(0, 0, HALF, ha[:, :HALF])
+
+        wb1 = [cast_a(ve, raw1[g], "wb1%d" % g) for g in range(PASSES)]
+        for g in range(PASSES):
+            c, s = quant(wb1[g][:], "w1%d" % g)
+            wq[1, g] = (c[:], s[:])
+        acc01 = bank(1, "acc01")
+        first_product(acc01[:, :HALF], 0, HALF, S)
+        first_product(acc01[:, HALF:], 1, 0, HALF)
+        acc1 = bank(6, "acc1b")
+        first_product(acc1[:, :HALF], 1, HALF, S)
+        nc.scalar.activation(ha[:, HALF : HALF + S], acc01[:], GELU)
+        nc.scalar.activation(ha[:, HALF + S :], acc1[:, :HALF], GELU)
+        scatter_s(0, HALF, S, ha[:, HALF:S])
+
+        for g in range(PASSES):
+            wbb = cast_b(ve, rawb[g], "wbb%d" % g)
+            c, s = quant(wbb[:], "wb%d" % g)
+            for u in range(2):
+                wq[2 + u, g] = (c[:, P * u : P * (u + 1)], s[:, P * u : P * (u + 1)])
+        scatter_v(1, 0, S, ha[:, S:])
+
+        def late_products(a, b):
+            acc = bank(b, "accb%d" % a)
+            for u in range(2):
+                first_product(acc[:, HALF * u : HALF * (u + 1)], 2 + u, HALF * a, HALF * (a + 1))
+            h = tile([P, S], F32, "hb%d" % a)
+            nc.scalar.activation(h[:], acc[:], GELU)
+            return h
+
+        hb0 = late_products(0, 7)
+        scatter_s(2, 0, HALF, hb0[:, :HALF])
+        scatter_v(3, 0, HALF, hb0[:, HALF:])
+
+        def turn_sum_a(w, banks):
+            tiles = [bank(b, "zT%d%d" % (w, b)) for b in banks]
+            for src, first in ((sk[w], True), (win[w], False)):
+                for vt in range(8):
+                    s = vt % 4
+                    turn(
+                        tiles[vt // 4][:, P * s : P * (s + 1)],
+                        src[:, P * vt : P * (vt + 1)],
+                        first and s == 0,
+                        not first and s == 3,
+                    )
+            return tiles
+
+        zta = [tile([P, 2, 4, P], BF16, "zta%d" % c) for c in range(2)]
+
+        def round_a(copy, w, src, c):
             copy(
-                z.bitcast(F32).rearrange("p (v u) -> p v u", u=2),
-                back[:, : 256 * pairs].rearrange("p (u v) -> p v u", u=2),
+                zta[c][:, :, :, 64 * w : 64 * (w + 1)].rearrange("v u b (r e) -> v u b r e", e=2),
+                src[:].rearrange("v (b r u e) -> v u b r e", b=4, u=2, e=2),
             )
 
-        def quant_z(z, name, words):
-            zc = tile([P, words], U32, "c" + name)
-            zs = tile([P, words], U8, "s" + name)
-            nc.vector.quantize_mx(out=zc[:].bitcast(FP8X4), scales=zs[:], in_=z)
-            return zc, zs
+        t0 = turn_sum_a(0, (2, 3))
+        tb = [bank(b, "zTb%d" % b) for b in (0, 1, 6, 7)]
+        t1 = turn_sum_a(1, (4, 5))
 
-        def second_product(res, j, h, zc, zs, s_from, first, last):
+        def turn_b(j, srcs, first):
+            for u in range(2):
+                for G in range(2):
+                    at = P * (2 * u + G)
+                    cells = slice(256 * j + P * G, 256 * j + P * (G + 1))
+                    turn(tb[j][:, at : at + P], srcs[2 + u][:, cells], first and at == 0, not first and at == 3 * P)
+
+        for c in range(2):
+            round_a(sc, 0, t0[c], c)
+        round_a(sc, 1, t1[0], 0)
+        round_a(ve, 1, t1[1], 1)
+        hb1 = late_products(1, 2)
+        for j in range(4):
+            turn_b(j, sk, True)
+        scatter_s(2, HALF, S, hb1[:, :HALF])
+        scatter_v(3, HALF, S, hb1[:, HALF:])
+
+        def weave(copy, back, z, words):
+            copy(
+                z.bitcast(F32).rearrange("p (v u) -> p v u", u=2),
+                back[:, :words].rearrange("p (u v) -> p v u", u=2),
+            )
+
+        def second_product(res, h, zq, s, first, last):
             for G in range(2):
                 nc.tensor.matmul_mx(
                     out=res[:, P * G : P * (G + 1)],
                     lhsT=w2w[:, h, G, :].bitcast(FP4X4),
                     lhsT_scale=w2s[:, h, :],
-                    rhs=zc[:, P * s_from : P * (s_from + 1)].bitcast(FP8X4),
-                    rhs_scale=zs[:, P * s_from : P * (s_from + 1)],
+                    rhs=zq[0][:, P * s : P * (s + 1)].bitcast(FP8X4),
+                    rhs_scale=zq[1][:, P * s : P * (s + 1)],
                     start=(first and G == 0),
                     stop=(last and G == 1),
                 )
 
-        za = [tile([P, 1024], BF16, "za%d" % c) for c in range(2)]
+        za = []
+        for c in range(2):
+            back = bank(3 + c, "backa%d" % c)
+            for u in range(2):
+                for s in range(2):
+                    at = P * (2 * u + s)
+                    pairs = zta[c][:, u, 2 * s : 2 * s + 2, :].rearrange("v g m -> v (g m)")
+                    nc.tensor.transpose(back[:, at : at + P], pairs.bitcast(F32), ident[:])
+            z = tile([P, 1024], BF16, "za%d" % c)
+            weave((sc, ve)[c], back, z[:], 512)
+            za.append(z)
+        for j in range(4):
+            turn_b(j, win, False)
+        qa = [quant(za[c][:], "za%d" % c) for c in range(2)]
+        res = [bank(b, "res%d" % b) for b in (2, 5, 3, 4)]
 
-        def finish_a(c):
-            back = bank(2 + c, "backa%d" % c)
-            for s in range(2):
-                for u in range(2):
-                    turn_back(back, zta[c][:, s, u].rearrange("v g m -> v (g m)"), s, u, 2)
-            weave(nc.scalar.copy, back, za[c][:], 2)
-
-        finish_a(0)
-        qa = [quant_z(za[0][:], "za0", 256)]
-        gelu_scatter(3, HALF, S, acc3[1][:, :HALF], "wb3")
-        finish_a(1)
-
-        def round_b(copy, src, pairs, name):
-            zt = tile([P, 256 * pairs], BF16, name)
-            copy(zt[:], src[:, : 256 * pairs])
-            return zt
-
-        t2 = turn_sum(2, (5, 4))
-        zt2 = [round_b(nc.scalar.copy, t2[c], 2, "zt2%d" % c) for c in range(2)]
-        def pairs_of_window_2(j):
-            return zt2[j // 2][:, 256 * (j % 2) : 256 * (j % 2 + 1)]
-
-        backb = [bank(2 + j, "backb%d" % j) for j in range(2)]
-        for j in range(2):
-            turn_back(backb[j], pairs_of_window_2(j), 0, 0, 1)
-        res = [bank(b, "res%d" % b) for b in (1, 7)]
-        for j in range(2):
-            second_product(res[j], j, 0, qa[0][0], qa[0][1], j, True, False)
-        order = (2, 3, 0, 1)
-        t3_bank = {2: 0, 3: 6, 0: 5, 1: 4}
-        t3 = {j: bank(t3_bank[j], "zT3%d" % j) for j in order}
-        for src, first in ((sk[3], True), (win[3], False)):
-            for j in order:
-                turn([(t3[j], 2)], src[:, 256 * j : 256 * (j + 1)], first)
-
-        sc, ve = nc.scalar.copy, nc.vector.tensor_copy
-        qa.append(quant_z(za[1][:], "za1", 256))
-        backb = {j: backb[j] for j in range(2)}
-        res = {j: res[j] for j in range(2)}
-        for i, j in enumerate(order):
-            zt = round_b((sc, ve, sc, ve)[i], t3[j], 1, "zt3%d" % j)
-            if j >= 2:
-                backb[j] = bank(t3_bank[j], "backb%d" % j)
-                turn_back(backb[j], pairs_of_window_2(j), 0, 0, 1)
-            turn_back(backb[j], zt[:], 0, 1, 1)
-        zb = {j: tile([P, 512], BF16, "zb%d" % j) for j in order}
-        for i, j in enumerate(order):
-            weave((sc, ve, sc, sc)[i], backb[j], zb[j][:], 1)
-        for j in (2, 3):
-            res[j] = bank(t3_bank[j - 2], "res%d" % j)
-            second_product(res[j], j, 0, qa[1][0], qa[1][1], j - 2, True, False)
-        for j in order:
-            zc, zs = quant_z(zb[j][:], "zb%d" % j, P)
-            second_product(res[j], j, 1, zc, zs, 0, False, True)
-        for i, j in enumerate(order):
+        zb = []
+        for j in range(4):
+            zt = tile([P, 512], BF16, "ztb%d" % j)
+            (sc, ve, sc, ve)[j](zt[:], tb[j][:])
+            back = bank((0, 1, 6, 7)[j], "backb%d" % j)
+            for u in range(2):
+                nc.tensor.transpose(back[:, P * u : P * (u + 1)], zt[:, 256 * u : 256 * (u + 1)].bitcast(F32), ident[:])
+            z = tile([P, 512], BF16, "zb%d" % j)
+            weave((sc, sc, sc, ve)[j], back, z[:], 256)
+            zb.append(z)
+        for j in range(4):
+            second_product(res[j], 0, qa[j // 2], j % 2, True, False)
+        for j in range(4):
+            second_product(res[j], 1, quant(zb[j][:], "zb%d" % j), 0, False, True)
+        for j in range(4):
             o = tile([P, 256], F32, "o%d" % j)
-            (sc, ve, sc, ve)[i](o[:], res[j][:, :256])
+            (sc, ve, sc, ve)[j](o[:], res[j][:, :256])
             nc.sync.dma_start(out[:, 256 * j : 256 * (j + 1)], o[:])

@@ -76,9 +76,8 @@ def tile_picked_unet_gelu_p_kernel(
             load_scales(g)
             load_x(g, 0, T)
         nc.sync.dma_start(cell_sb[:], cell)
-        rawb = [load_w("rawb", 0, 2 * P, 2 * P)]
         raw1 = [load_w("raw1", g, P, P) for g in range(PASSES)]
-        rawb.append(load_w("rawb", 1, 2 * P, 2 * P))
+        rawb = [load_w("rawb", g, 2 * P, 2 * P) for g in range(PASSES)]
         sk = [load_skip(w) for w in range(4)]
         w2w = tile([P, 2, 2, 2 * N], U8, "w2w")
         w2s = tile([P, 2, N], U8, "w2s")
@@ -164,44 +163,58 @@ def tile_picked_unet_gelu_p_kernel(
         def turn(dst, src, start, stop):
             nc.tensor.matmul(dst, src, ident[:], is_transpose=True, start=start, stop=stop)
 
-        ha = tile([P, 2 * S], F32, "ha")
-        for i, b in enumerate((0, 7)):
-            acc = bank(b, "acc0a%d" % i)
-            first_product(acc[:, :P], 0, P * i, P * (i + 1))
-            nc.scalar.activation(ha[:, P * i : P * (i + 1)], acc[:, :P], GELU)
-        scatter_s(0, 0, HALF, ha[:, :HALF])
+        def gelu(h, acc):
+            nc.scalar.activation(h, acc, GELU)
 
-        wb1 = [cast_a(ve, raw1[g], "wb1%d" % g) for g in range(PASSES)]
-        for g in range(PASSES):
-            c, s = quant(wb1[g][:], "w1%d" % g)
+        MOST = S - P
+        h0a = tile([P, P], F32, "h0a")
+        acc = bank(0, "acc0a")
+        first_product(acc[:, :P], 0, 0, P)
+        gelu(h0a[:], acc[:, :P])
+
+        def quant_w1(g, copy):
+            c, s = quant(cast_a(copy, raw1[g], "wb1%d" % g)[:], "w1%d" % g)
             wq[1, g] = (c[:], s[:])
-        acc01 = bank(1, "acc01")
-        first_product(acc01[:, :HALF], 0, HALF, S)
-        first_product(acc01[:, HALF:], 1, 0, HALF)
-        acc1 = bank(6, "acc1b")
-        first_product(acc1[:, :HALF], 1, HALF, S)
-        nc.scalar.activation(ha[:, HALF : HALF + S], acc01[:], GELU)
-        nc.scalar.activation(ha[:, HALF + S :], acc1[:, :HALF], GELU)
-        scatter_s(0, HALF, S, ha[:, HALF:S])
 
+        quant_w1(0, ve)
+        scatter_v(0, 0, P, h0a[:])
+        quant_w1(1, sc)
+        acc = bank(6, "acc0b")
+        first_product(acc[:, :P], 0, P, HALF)
+        first_product(acc[:, P:HALF], 0, HALF, MOST)
+        h0b = tile([P, HALF], F32, "h0b", "raw11")
+        gelu(h0b[:], acc[:, :HALF])
+        scatter_v(0, P, MOST, h0b[:])
+
+        wbb = [cast_b(sc, rawb[g], "wbb%d" % g) for g in range(PASSES)]
         for g in range(PASSES):
-            wbb = cast_b(ve, rawb[g], "wbb%d" % g)
-            c, s = quant(wbb[:], "wb%d" % g)
+            c, s = quant(wbb[g][:], "wb%d" % g)
             for u in range(2):
                 wq[2 + u, g] = (c[:, P * u : P * (u + 1)], s[:, P * u : P * (u + 1)])
-        scatter_v(1, 0, S, ha[:, S:])
+        acc01 = bank(1, "acc01")
+        first_product(acc01[:, :P], 0, MOST, S)
+        first_product(acc01[:, P:MOST], 1, 0, HALF)
+        acc1 = bank(0, "acc1b")
+        first_product(acc1[:, :HALF], 1, HALF, S)
+        ha = tile([P, P + S], F32, "ha", "rawb1")
+        gelu(ha[:, :MOST], acc01[:, :MOST])
+        gelu(ha[:, MOST:], acc1[:, :HALF])
+        scatter_s(0, MOST, S, ha[:, :P])
+        scatter_v(1, 0, S, ha[:, P:])
 
-        def late_products(a, b):
-            acc = bank(b, "accb%d" % a)
-            for u in range(2):
-                first_product(acc[:, HALF * u : HALF * (u + 1)], 2 + u, HALF * a, HALF * (a + 1))
-            h = tile([P, S], F32, "hb%d" % a)
-            nc.scalar.activation(h[:], acc[:], GELU)
+        def hidden(b, w, halves):
+            acc = bank(b, "acc%d%d" % (w, halves[0]))
+            for i, a in enumerate(halves):
+                first_product(acc[:, HALF * i : HALF * (i + 1)], w, HALF * a, HALF * (a + 1))
+            h = tile([P, HALF * len(halves)], F32, "h%d%d" % (w, halves[0]))
+            gelu(h[:], acc[:, : HALF * len(halves)])
             return h
 
-        hb0 = late_products(0, 7)
-        scatter_s(2, 0, HALF, hb0[:, :HALF])
-        scatter_v(3, 0, HALF, hb0[:, HALF:])
+        h2a = hidden(7, 2, (0,))
+        h3 = hidden(1, 3, (0, 1))
+        scatter_s(2, 0, HALF, h2a[:])
+        scatter_v(3, 0, S, h3[:])
+        h2b = hidden(6, 2, (1,))
 
         def turn_sum_a(w, banks):
             tiles = [bank(b, "zT%d%d" % (w, b)) for b in banks]
@@ -225,25 +238,26 @@ def tile_picked_unet_gelu_p_kernel(
             )
 
         t0 = turn_sum_a(0, (2, 3))
-        tb = [bank(b, "zTb%d" % b) for b in (0, 1, 6, 7)]
         t1 = turn_sum_a(1, (4, 5))
 
-        def turn_b(j, srcs, first):
-            for u in range(2):
+        tb = [bank(b, "zTb%d" % b) for b in (0, 7, 6, 1)]
+
+        def turn_b(u, src, first):
+            for j in range(4):
                 for G in range(2):
                     at = P * (2 * u + G)
                     cells = slice(256 * j + P * G, 256 * j + P * (G + 1))
-                    turn(tb[j][:, at : at + P], srcs[2 + u][:, cells], first and at == 0, not first and at == 3 * P)
+                    turn(tb[j][:, at : at + P], src[:, cells], first and at == 0, not first and at == 3 * P)
 
+        round_a(sc, 0, t0[0], 0)
+        scatter_s(2, HALF, S, h2b[:])
+        round_a(sc, 0, t0[1], 1)
         for c in range(2):
-            round_a(sc, 0, t0[c], c)
-        round_a(sc, 1, t1[0], 0)
-        round_a(ve, 1, t1[1], 1)
-        hb1 = late_products(1, 2)
-        for j in range(4):
-            turn_b(j, sk, True)
-        scatter_s(2, HALF, S, hb1[:, :HALF])
-        scatter_v(3, HALF, S, hb1[:, HALF:])
+            round_a(sc, 1, t1[c], c)
+        for u in range(2):
+            turn_b(u, sk[2 + u], True)
+        for u in range(2):
+            turn_b(u, win[2 + u], False)
 
         def weave(copy, back, z, words):
             copy(
@@ -265,25 +279,23 @@ def tile_picked_unet_gelu_p_kernel(
 
         za = []
         for c in range(2):
-            back = bank(3 + c, "backa%d" % c)
+            back = bank(2 + c, "backa%d" % c)
             for u in range(2):
                 for s in range(2):
                     at = P * (2 * u + s)
                     pairs = zta[c][:, u, 2 * s : 2 * s + 2, :].rearrange("v g m -> v (g m)")
                     nc.tensor.transpose(back[:, at : at + P], pairs.bitcast(F32), ident[:])
             z = tile([P, 1024], BF16, "za%d" % c)
-            weave((sc, ve)[c], back, z[:], 512)
+            weave((ve, sc)[c], back, z[:], 512)
             za.append(z)
-        for j in range(4):
-            turn_b(j, win, False)
         qa = [quant(za[c][:], "za%d" % c) for c in range(2)]
-        res = [bank(b, "res%d" % b) for b in (2, 5, 3, 4)]
+        res = [bank(b, "res%d" % b) for b in (4, 5, 2, 3)]
 
         zb = []
         for j in range(4):
             zt = tile([P, 512], BF16, "ztb%d" % j)
             (sc, ve, sc, ve)[j](zt[:], tb[j][:])
-            back = bank((0, 1, 6, 7)[j], "backb%d" % j)
+            back = bank((0, 7, 6, 1)[j], "backb%d" % j)
             for u in range(2):
                 nc.tensor.transpose(back[:, P * u : P * (u + 1)], zt[:, 256 * u : 256 * (u + 1)].bitcast(F32), ident[:])
             z = tile([P, 512], BF16, "zb%d" % j)

@@ -1,7 +1,6 @@
 from contextlib import ExitStack
 
 import concourse.mybir as mybir
-from concourse.masks import make_identity
 
 K, T, S, H, N, U = 1024, 2048, 512, 512, 128, 1024
 FLOPS = 2 * K * H * S + 2 * H * N * U
@@ -16,10 +15,12 @@ FP8X4 = mybir.dt.float8_e4m3fn_x4
 FP4X4 = mybir.dt.float4_e2m1fn_x4
 GELU = mybir.ActivationFunctionType.Gelu_apprx_tanh
 COPY = mybir.ActivationFunctionType.Copy
+ADD = mybir.AluOpType.add
 
 P = 128
 PASSES = K // 512
-HALF = S // 2
+FIRST = 128
+STRETCH = 256
 
 
 def tile_picked_unet_gelu_p_kernel(
@@ -41,66 +42,50 @@ def tile_picked_unet_gelu_p_kernel(
         cell_sb = lists.tile([P, S // 16], U16, name="cell_sb")
         xs = tile([P, T], U8, "xs")
         nc.gpsimd.memset(xs[:].bitcast(I32), 0)
+        w2s = tile([P, N], U8, "w2s")
+        nc.gpsimd.memset(w2s[:].bitcast(I32), 0)
 
-        w_rows = w1.rearrange("(g k j) c -> g k j c", g=PASSES, j=4)
-
-        def load_w(name, g, c0, width):
-            raw = tile([P, 4, width], F32, "%s%d" % (name, g))
-            nc.sync.dma_start(raw[:], w_rows[g][:, :, c0 : c0 + width])
-            return raw
-
-        def load_skip(w):
-            sk = tile([P, U], F32, "skip%d" % w)
-            if w < 2:
-                rows = skip[P * w : P * (w + 1), :]
-            else:
-                rows = skip[2 * P :, :].rearrange("(r u e) v -> u r e v", u=2, e=2)[w - 2]
-            nc.sync.dma_start(sk[:], rows)
-            return sk
-
+        raw = [tile([P, 4, H], F32, "raw%d" % g) for g in range(PASSES)]
         xw = [tile([P, T], U32, "xw%d" % g) for g in range(PASSES)]
+        skp = [tile([P, 2, U], F32, "skip%d" % u) for u in range(2)]
+        w2w = tile([P, 2 * N], U8, "w2w")
 
-        def load_x(g, lo, hi):
-            nc.sync.dma_start(
-                xw[g][:, lo:hi].bitcast(I32), x_words[g].rearrange("p n t -> p (n t)").bitcast(I32)[:, lo:hi]
-            )
+        def load_w(g):
+            nc.sync.dma_start(raw[g][:], w1.rearrange("(g k j) c -> g k j c", g=PASSES, j=4)[g])
 
-        def load_scales(g):
-            for q in range(4):
+        def load_x(g):
+            nc.sync.dma_start(xw[g][:].bitcast(I32), x_words[g].rearrange("p n t -> p (n t)").bitcast(I32))
+
+        def load_scales(first, last):
+            for r in range(first, last):
+                g, q = divmod(r, 4)
                 at = 32 * q + 4 * g
                 nc.sync.dma_start(xs[at : at + 4, :].bitcast(I32), x_scales[g, 4 * q : 4 * q + 4, :].bitcast(I32))
 
-        raw0 = [load_w("raw0", g, 0, P) for g in range(PASSES)]
+        def load_skip(u):
+            nc.sync.dma_start(skp[u][:], skip.rearrange("(p u e) v -> u p e v", u=2, e=2)[u])
+
+        load_w(0)
         nc.sync.dma_start(offs_sb[:], offs)
-        for g in range(PASSES):
-            load_scales(g)
-            load_x(g, 0, T)
         nc.sync.dma_start(cell_sb[:], cell)
-        raw1 = [load_w("raw1", g, P, P) for g in range(PASSES)]
-        rawb = [load_w("rawb", g, 2 * P, 2 * P) for g in range(PASSES)]
-        sk = [load_skip(w) for w in range(4)]
-        w2w = tile([P, 2, 2, 2 * N], U8, "w2w")
-        w2s = tile([P, 2, N], U8, "w2s")
-        nc.vector.memset(w2w[:].bitcast(I32), 0)
-        nc.vector.memset(w2s[:].bitcast(I32), 0)
-        for G in range(2):
-            nc.sync.dma_start(
-                w2w[64 * G : 64 * (G + 1), :, G, :].bitcast(I32),
-                w2_words[0].rearrange("(h r) c -> r h c", h=2).bitcast(I32),
-            )
+        load_scales(0, 3)
+        load_x(0)
+        load_scales(3, 8)
+        load_w(1)
+        load_x(1)
+        load_skip(0)
+        nc.sync.dma_start(w2w[:].bitcast(I32), w2_words[0].bitcast(I32))
         for q in range(4):
             nc.sync.dma_start(
-                w2s[32 * q : 32 * q + 4, :, :].bitcast(I32),
-                w2_scales[0].rearrange("(h q a) c -> q a h c", h=2, q=2)[q % 2].bitcast(I32),
+                w2s[32 * q : 32 * q + 4, :].bitcast(I32), w2_scales[0, 4 * q : 4 * q + 4, :].bitcast(I32)
             )
+        load_skip(1)
 
-        ident = tile([P, P], F32, "ident")
-        make_identity(nc, ident[:])
-        win = [tile([P, U], F32, "win%d" % w) for w in range(4)]
+        win = [tile([P, U], F32, "win%d" % t) for t in range(4)]
         nc.vector.memset(win[0][:], 0.0)
         nc.scalar.activation(win[1][:], win[0][:], GELU)
-        for w in (2, 3):
-            nc.vector.memset(win[w][:], 0.0)
+        for t in (2, 3):
+            nc.vector.memset(win[t][:], 0.0)
 
         sc, ve = nc.scalar.copy, nc.vector.tensor_copy
 
@@ -111,201 +96,137 @@ def tile_picked_unet_gelu_p_kernel(
             nc.vector.quantize_mx(out=codes[:].bitcast(FP8X4), scales=scales[:], in_=src)
             return codes, scales
 
-        def cast_a(copy, raw, name):
-            wb = tile([P, 512], BF16, name)
+        def cast(copy, g, lo, hi):
+            wb = tile([P, (hi - lo) * H], BF16, "wb%d%d" % (g, lo))
             copy(
-                wb[:].rearrange("k (c i j) -> k c j i", i=4, j=4),
-                raw[:].rearrange("k j (c i) -> k c j i", i=4),
-            )
-            return wb
-
-        def cast_b(copy, raw, name):
-            wb = tile([P, 1024], BF16, name)
-            copy(
-                wb[:].rearrange("k (u r e j) -> k r j u e", u=2, e=2, j=4),
-                raw[:].rearrange("k j (r u e) -> k r j u e", u=2, e=2),
+                wb[:].rearrange("k (t m j) -> k m j t", m=P, j=4),
+                raw[g][:].rearrange("k j (m t) -> k m j t", t=4)[:, :, :, lo:hi],
             )
             return wb
 
         wq = {}
-        wb0 = [cast_a(sc, raw0[g], "wb0%d" % g) for g in range(PASSES)]
-        for g in range(PASSES):
-            c, s = quant(wb0[g][:], "w0%d" % g)
-            wq[0, g] = (c[:], s[:])
+
+        def quant_w(wb, g, lo, hi):
+            codes, scales = quant(wb[:], "w%d%d" % (g, lo))
+            for t in range(lo, hi):
+                cols = slice(P * (t - lo), P * (t - lo + 1))
+                wq[g, t] = (codes[:, cols], scales[:, cols])
 
         xsg = tile([P, S], U8, "xsg")
-        xg0 = tile([P, S], U32, "xg0")
-        xg1 = [tile([P, HALF], U32, "xg1%d" % a) for a in range(2)]
+        xg = [tile([P, S], U32, "xg%d" % g) for g in range(PASSES)]
+        quant_w(cast(sc, 0, 0, 4), 0, 0, 4)
         nc.vector.tensor_copy(xsg[:], xs[:].indirect(offs_sb[:]))
-        nc.vector.tensor_copy(xg0[:], xw[0][:].indirect(offs_sb[:]))
-        for a in range(2):
-            nc.vector.tensor_copy(xg1[a][:], xw[1][:].indirect(offs_sb[:, 16 * a : 16 * (a + 1)]))
+        nc.vector.tensor_copy(xg[0][:], xw[0][:].indirect(offs_sb[:]))
+        early, late = cast(sc, 1, 0, 2), cast(ve, 1, 2, 4)
+        quant_w(early, 1, 0, 2)
+        quant_w(late, 1, 2, 4)
+        nc.vector.tensor_copy(xg[1][:, :FIRST], xw[1][:].indirect(offs_sb[:, : FIRST // 16]))
+        nc.vector.tensor_copy(xg[1][:, FIRST:], xw[1][:].indirect(offs_sb[:, FIRST // 16 :]))
 
-        def first_product(acc, w, lo, hi):
-            for g in range(PASSES):
-                words = xg0[:, lo:hi] if g == 0 else xg1[lo // HALF][:, lo % HALF : lo % HALF + hi - lo]
+        groups = [
+            [(0, 0, FIRST), (1, 0, FIRST)],
+            [(0, FIRST, 256), (0, 256, S)],
+            [(1, FIRST, 256), (1, 256, S)],
+            [(3, 0, S)],
+            [(2, 0, S)],
+        ]
+        acc = [bank(b, "acc%d" % b) for b in range(len(groups) - 1)]
+
+        def product(b, g):
+            at = 0
+            for i, (t, lo, hi) in enumerate(groups[b]):
                 nc.tensor.matmul_mx(
-                    out=acc,
-                    lhsT=wq[w, g][0].bitcast(FP8X4),
-                    lhsT_scale=wq[w, g][1],
-                    rhs=words.bitcast(FP8X4),
+                    out=acc[b][:, at : at + hi - lo],
+                    lhsT=wq[g, t][0].bitcast(FP8X4),
+                    lhsT_scale=wq[g, t][1],
+                    rhs=xg[g][:, lo:hi].bitcast(FP8X4),
                     rhs_scale=xsg[4 * g : P, lo:hi],
-                    start=(g == 0),
-                    stop=(g == PASSES - 1),
+                    start=(g == 0 and i == 0),
+                    stop=(g == PASSES - 1 and i == len(groups[b]) - 1),
                 )
+                at = at + hi - lo
 
-        def scatter_s(w, lo, hi, h):
-            nc.scalar.activation(win[w][:].indirect(cell_sb[:, lo // 16 : hi // 16]), h, COPY)
-
-        def scatter_v(w, lo, hi, h):
-            nc.vector.tensor_copy(win[w][:].indirect(cell_sb[:, lo // 16 : hi // 16]), h)
-
-        def turn(dst, src, start, stop):
-            nc.tensor.matmul(dst, src, ident[:], is_transpose=True, start=start, stop=stop)
-
-        def gelu(h, acc):
-            nc.scalar.activation(h, acc, GELU)
-
-        MOST = S - P
-        h0a = tile([P, P], F32, "h0a")
-        acc = bank(0, "acc0a")
-        first_product(acc[:, :P], 0, 0, P)
-        gelu(h0a[:], acc[:, :P])
-
-        def quant_w1(g, copy):
-            c, s = quant(cast_a(copy, raw1[g], "wb1%d" % g)[:], "w1%d" % g)
-            wq[1, g] = (c[:], s[:])
-
-        quant_w1(0, ve)
-        scatter_v(0, 0, P, h0a[:])
-        quant_w1(1, sc)
-        acc = bank(6, "acc0b")
-        first_product(acc[:, :P], 0, P, HALF)
-        first_product(acc[:, P:HALF], 0, HALF, MOST)
-        h0b = tile([P, HALF], F32, "h0b", "raw11")
-        gelu(h0b[:], acc[:, :HALF])
-        scatter_v(0, P, MOST, h0b[:])
-
-        wbb = [cast_b(sc, rawb[g], "wbb%d" % g) for g in range(PASSES)]
         for g in range(PASSES):
-            c, s = quant(wbb[g][:], "wb%d" % g)
-            for u in range(2):
-                wq[2 + u, g] = (c[:, P * u : P * (u + 1)], s[:, P * u : P * (u + 1)])
-        acc01 = bank(1, "acc01")
-        first_product(acc01[:, :P], 0, MOST, S)
-        first_product(acc01[:, P:MOST], 1, 0, HALF)
-        acc1 = bank(0, "acc1b")
-        first_product(acc1[:, :HALF], 1, HALF, S)
-        ha = tile([P, P + S], F32, "ha", "rawb1")
-        gelu(ha[:, :MOST], acc01[:, :MOST])
-        gelu(ha[:, MOST:], acc1[:, :HALF])
-        scatter_s(0, MOST, S, ha[:, :P])
-        scatter_v(1, 0, S, ha[:, P:])
+            for b in range(len(acc)):
+                product(b, g)
 
-        def hidden(b, w, halves):
-            acc = bank(b, "acc%d%d" % (w, halves[0]))
-            for i, a in enumerate(halves):
-                first_product(acc[:, HALF * i : HALF * (i + 1)], w, HALF * a, HALF * (a + 1))
-            h = tile([P, HALF * len(halves)], F32, "h%d%d" % (w, halves[0]))
-            gelu(h[:], acc[:, : HALF * len(halves)])
+        def gelu(b):
+            width = sum(hi - lo for t, lo, hi in groups[b])
+            h = tile([P, width], F32, "h%d" % b)
+            nc.scalar.activation(h[:], acc[b][:, :width], GELU)
             return h
 
-        h2a = hidden(7, 2, (0,))
-        h3 = hidden(1, 3, (0, 1))
-        scatter_s(2, 0, HALF, h2a[:])
-        scatter_v(3, 0, S, h3[:])
-        h2b = hidden(6, 2, (1,))
+        def scatter_s(t, lo, hi, h):
+            nc.scalar.activation(win[t][:].indirect(cell_sb[:, lo // 16 : hi // 16]), h, COPY)
 
-        def turn_sum_a(w, banks):
-            tiles = [bank(b, "zT%d%d" % (w, b)) for b in banks]
-            for src, first in ((sk[w], True), (win[w], False)):
-                for vt in range(8):
-                    s = vt % 4
-                    turn(
-                        tiles[vt // 4][:, P * s : P * (s + 1)],
-                        src[:, P * vt : P * (vt + 1)],
-                        first and s == 0,
-                        not first and s == 3,
-                    )
-            return tiles
+        def scatter_v(t, lo, hi, h):
+            nc.vector.tensor_copy(win[t][:].indirect(cell_sb[:, lo // 16 : hi // 16]), h)
 
-        zta = [tile([P, 2, 4, P], BF16, "zta%d" % c) for c in range(2)]
+        h = gelu(0)
+        acc.append(bank(0, "acc4"))
+        for g in range(PASSES):
+            product(4, g)
+        scatter_v(0, 0, FIRST, h[:, :FIRST])
+        scatter_s(1, 0, FIRST, h[:, FIRST:])
+        scatter_v(0, FIRST, S, gelu(1)[:])
+        h1 = gelu(2)
+        h3 = gelu(3)
+        scatter_v(3, 0, FIRST, h3[:, :FIRST])
+        h2 = gelu(4)
+        scatter_s(1, FIRST, S, h1[:])
+        scatter_v(2, 0, S, h2[:])
+        scatter_s(3, FIRST, S, h3[:, FIRST:])
 
-        def round_a(copy, w, src, c):
+        planes = [tile([P, 4, STRETCH], BF16, "planes%d" % s) for s in range(4)]
+
+        def add(engine, t, s):
+            cells = slice(STRETCH * s, STRETCH * (s + 1))
+            engine.tensor_tensor(planes[s][:, t, :], win[t][:, cells], skp[t // 2][:, t % 2, cells], ADD)
+
+        for s in range(4):
+            add(nc.gpsimd, 0, s)
+        for s in range(4):
+            add(nc.gpsimd, 1, s)
+        for s in range(4):
+            add(nc.vector, 2, s)
+            add(nc.vector, 3, s)
+
+        def weave(copy, s):
+            z = tile([P, 4 * STRETCH], BF16, "z%d" % s)
             copy(
-                zta[c][:, :, :, 64 * w : 64 * (w + 1)].rearrange("v u b (r e) -> v u b r e", e=2),
-                src[:].rearrange("v (b r u e) -> v u b r e", b=4, u=2, e=2),
+                z[:].rearrange("p (c i t) -> p c t i", i=4, t=4),
+                planes[s][:].rearrange("p t (c i) -> p c t i", i=4),
             )
+            return z
 
-        t0 = turn_sum_a(0, (2, 3))
-        t1 = turn_sum_a(1, (4, 5))
-
-        tb = [bank(b, "zTb%d" % b) for b in (0, 7, 6, 1)]
-
-        def turn_b(u, src, first):
-            for j in range(4):
-                for G in range(2):
-                    at = P * (2 * u + G)
-                    cells = slice(256 * j + P * G, 256 * j + P * (G + 1))
-                    turn(tb[j][:, at : at + P], src[:, cells], first and at == 0, not first and at == 3 * P)
-
-        round_a(sc, 0, t0[0], 0)
-        scatter_s(2, HALF, S, h2b[:])
-        round_a(sc, 0, t0[1], 1)
-        for c in range(2):
-            round_a(sc, 1, t1[c], c)
-        for u in range(2):
-            turn_b(u, sk[2 + u], True)
-        for u in range(2):
-            turn_b(u, win[2 + u], False)
-
-        def weave(copy, back, z, words):
-            copy(
-                z.bitcast(F32).rearrange("p (v u) -> p v u", u=2),
-                back[:, :words].rearrange("p (u v) -> p v u", u=2),
+        def finish(copy, s, z):
+            codes, scales = quant(z[:], "z%d" % s)
+            res = bank((4, 5, 6, 7)[s], "res%d" % s)
+            nc.tensor.matmul_mx(
+                out=res[:, :STRETCH],
+                lhsT=w2w[:].bitcast(FP4X4),
+                lhsT_scale=w2s[:],
+                rhs=codes[:].bitcast(FP8X4),
+                rhs_scale=scales[:],
+                start=True,
+                stop=True,
             )
+            return res
 
-        def second_product(res, h, zq, s, first, last):
-            for G in range(2):
-                nc.tensor.matmul_mx(
-                    out=res[:, P * G : P * (G + 1)],
-                    lhsT=w2w[:, h, G, :].bitcast(FP4X4),
-                    lhsT_scale=w2s[:, h, :],
-                    rhs=zq[0][:, P * s : P * (s + 1)].bitcast(FP8X4),
-                    rhs_scale=zq[1][:, P * s : P * (s + 1)],
-                    start=(first and G == 0),
-                    stop=(last and G == 1),
-                )
+        def store(copy, s, res):
+            o = tile([P, STRETCH], F32, "o%d" % s)
+            copy(o[:], res[:, :STRETCH])
+            nc.sync.dma_start(out[:, STRETCH * s : STRETCH * (s + 1)], o[:])
 
-        za = []
-        for c in range(2):
-            back = bank(2 + c, "backa%d" % c)
-            for u in range(2):
-                for s in range(2):
-                    at = P * (2 * u + s)
-                    pairs = zta[c][:, u, 2 * s : 2 * s + 2, :].rearrange("v g m -> v (g m)")
-                    nc.tensor.transpose(back[:, at : at + P], pairs.bitcast(F32), ident[:])
-            z = tile([P, 1024], BF16, "za%d" % c)
-            weave((ve, sc)[c], back, z[:], 512)
-            za.append(z)
-        qa = [quant(za[c][:], "za%d" % c) for c in range(2)]
-        res = [bank(b, "res%d" % b) for b in (4, 5, 2, 3)]
-
-        zb = []
-        for j in range(4):
-            zt = tile([P, 512], BF16, "ztb%d" % j)
-            (sc, ve, sc, ve)[j](zt[:], tb[j][:])
-            back = bank((0, 7, 6, 1)[j], "backb%d" % j)
-            for u in range(2):
-                nc.tensor.transpose(back[:, P * u : P * (u + 1)], zt[:, 256 * u : 256 * (u + 1)].bitcast(F32), ident[:])
-            z = tile([P, 512], BF16, "zb%d" % j)
-            weave((sc, sc, sc, ve)[j], back, z[:], 256)
-            zb.append(z)
-        for j in range(4):
-            second_product(res[j], 0, qa[j // 2], j % 2, True, False)
-        for j in range(4):
-            second_product(res[j], 1, quant(zb[j][:], "zb%d" % j), 0, False, True)
-        for j in range(4):
-            o = tile([P, 256], F32, "o%d" % j)
-            (sc, ve, sc, ve)[j](o[:], res[j][:, :256])
-            nc.sync.dma_start(out[:, 256 * j : 256 * (j + 1)], o[:])
+        z0 = weave(sc, 0)
+        z1 = weave(sc, 1)
+        z2 = weave(sc, 2)
+        z3 = weave(ve, 3)
+        r0 = finish(sc, 0, z0)
+        r1 = finish(sc, 1, z1)
+        r3 = finish(sc, 3, z3)
+        r2 = finish(sc, 2, z2)
+        store(sc, 0, r0)
+        store(sc, 1, r1)
+        store(sc, 3, r3)
+        store(ve, 2, r2)

@@ -20,7 +20,8 @@ ADD = mybir.AluOpType.add
 P = 128
 PASSES = K // 512
 FIRST = 128
-STRETCH = 256
+UNIT = 128
+STRETCHES = ((0, 1), (1, 3), (3, 5), (5, 7), (7, 8))
 
 
 def tile_picked_unet_gelu_p_kernel(
@@ -177,33 +178,39 @@ def tile_picked_unet_gelu_p_kernel(
         scatter_v(2, 0, S, h2[:])
         scatter_s(3, FIRST, S, h3[:, FIRST:])
 
-        planes = [tile([P, 4, STRETCH], BF16, "planes%d" % s) for s in range(4)]
+        planes = tile([P, 4 * U], BF16, "planes")
+        units = planes[:].rearrange("p (u t c) -> p u t c", t=4, c=UNIT)
 
-        def add(engine, t, s):
-            cells = slice(STRETCH * s, STRETCH * (s + 1))
-            engine.tensor_tensor(planes[s][:, t, :], win[t][:, cells], skp[t // 2][:, t % 2, cells], ADD)
+        def add(engine, t, lo, hi):
+            cells = slice(UNIT * lo, UNIT * hi)
+            engine.tensor_tensor(
+                units[:, lo:hi, t, :],
+                win[t][:, cells].rearrange("p (u c) -> p u c", c=UNIT),
+                skp[t // 2][:, t % 2, cells].rearrange("p (u c) -> p u c", c=UNIT),
+                ADD,
+            )
 
-        for s in range(4):
-            add(nc.gpsimd, 0, s)
-        for s in range(4):
-            add(nc.gpsimd, 1, s)
-        for s in range(4):
-            add(nc.vector, 2, s)
-            add(nc.vector, 3, s)
+        for t in range(2):
+            for lo in (0, 4):
+                add(nc.gpsimd, t, lo, lo + 4)
+        for lo, hi in STRETCHES:
+            add(nc.vector, 2, lo, hi)
+            add(nc.vector, 3, lo, hi)
 
         def weave(copy, s):
-            z = tile([P, 4 * STRETCH], BF16, "z%d" % s)
+            lo, hi = STRETCHES[s]
+            z = tile([P, 4 * UNIT * (hi - lo)], BF16, "z%d" % s)
             copy(
-                z[:].rearrange("p (c i t) -> p c t i", i=4, t=4),
-                planes[s][:].rearrange("p t (c i) -> p c t i", i=4),
+                z[:].rearrange("p (u c i t) -> p u c t i", u=hi - lo, i=4, t=4),
+                planes[:, 4 * UNIT * lo : 4 * UNIT * hi].rearrange("p (u t c i) -> p u c t i", u=hi - lo, t=4, i=4),
             )
             return z
 
         def finish(copy, s, z):
             codes, scales = quant(z[:], "z%d" % s)
-            res = bank((4, 5, 6, 7)[s], "res%d" % s)
+            res = bank((4, 5, 6, 7, 1)[s], "res%d" % s)
             nc.tensor.matmul_mx(
-                out=res[:, :STRETCH],
+                out=res[:, : codes.shape[1]],
                 lhsT=w2w[:].bitcast(FP4X4),
                 lhsT_scale=w2s[:],
                 rhs=codes[:].bitcast(FP8X4),
@@ -214,19 +221,23 @@ def tile_picked_unet_gelu_p_kernel(
             return res
 
         def store(copy, s, res):
-            o = tile([P, STRETCH], F32, "o%d" % s)
-            copy(o[:], res[:, :STRETCH])
-            nc.sync.dma_start(out[:, STRETCH * s : STRETCH * (s + 1)], o[:])
+            lo, hi = STRETCHES[s]
+            o = tile([P, UNIT * (hi - lo)], F32, "o%d" % s)
+            copy(o[:], res[:, : UNIT * (hi - lo)])
+            nc.sync.dma_start(out[:, UNIT * lo : UNIT * hi], o[:])
 
         z0 = weave(sc, 0)
         z1 = weave(sc, 1)
         z2 = weave(sc, 2)
-        z3 = weave(ve, 3)
+        z4 = weave(sc, 4)
         r0 = finish(sc, 0, z0)
         r1 = finish(sc, 1, z1)
-        r3 = finish(sc, 3, z3)
+        z3 = weave(ve, 3)
         r2 = finish(sc, 2, z2)
+        r3 = finish(sc, 3, z3)
+        r4 = finish(sc, 4, z4)
         store(sc, 0, r0)
         store(sc, 1, r1)
-        store(sc, 3, r3)
-        store(ve, 2, r2)
+        store(sc, 2, r2)
+        store(ve, 3, r3)
+        store(ve, 4, r4)

@@ -239,5 +239,5 @@ def tile_picked_unet_gelu_p_kernel(
         store(sc, 0, r0)
         store(sc, 1, r1)
         store(sc, 2, r2)
-        store(ve, 3, r3)
+        store(sc, 3, r3)
         store(ve, 4, r4)

@@ -48,7 +48,8 @@ def tile_picked_unet_gelu_p_kernel(
 
         raw = [tile([P, 4, H], F32, "raw%d" % g) for g in range(PASSES)]
         xw = [tile([P, T], U32, "xw%d" % g) for g in range(PASSES)]
-        skp = [tile([P, 2, U], F32, "skip%d" % u) for u in range(2)]
+        parts = ((0, 1, 0, U), (1, 2, 0, 6 * UNIT), (2, 4, 0, U), (1, 2, 6 * UNIT, U))
+        skp = [tile([P, t1 - t0, hi - lo], F32, "skip%d" % n) for n, (t0, t1, lo, hi) in enumerate(parts)]
         w2w = tile([P, 2 * N], U8, "w2w")
 
         def load_w(g):
@@ -64,7 +65,8 @@ def tile_picked_unet_gelu_p_kernel(
                 nc.sync.dma_start(xs[at : at + 4, :].bitcast(I32), x_scales[g, 4 * q : 4 * q + 4, :].bitcast(I32))
 
         def load_skip(u):
-            nc.sync.dma_start(skp[u][:], skip.rearrange("(p u e) v -> u p e v", u=2, e=2)[u])
+            t0, t1, lo, hi = parts[u]
+            nc.sync.dma_start(skp[u][:], skip.rearrange("(p t) v -> p t v", t=4)[:, t0:t1, lo:hi])
 
         load_w(0)
         nc.sync.dma_start(offs_sb[:], offs)
@@ -75,12 +77,14 @@ def tile_picked_unet_gelu_p_kernel(
         load_w(1)
         load_x(1)
         load_skip(0)
+        load_skip(1)
         nc.sync.dma_start(w2w[:].bitcast(I32), w2_words[0].bitcast(I32))
         for q in range(4):
             nc.sync.dma_start(
                 w2s[32 * q : 32 * q + 4, :].bitcast(I32), w2_scales[0, 4 * q : 4 * q + 4, :].bitcast(I32)
             )
-        load_skip(1)
+        load_skip(2)
+        load_skip(3)
 
         win = [tile([P, U], F32, "win%d" % t) for t in range(4)]
         nc.vector.memset(win[0][:], 0.0)
@@ -183,17 +187,20 @@ def tile_picked_unet_gelu_p_kernel(
 
         def add(engine, t, lo, hi):
             cells = slice(UNIT * lo, UNIT * hi)
+            n = [n for n, (t0, t1, a, b) in enumerate(parts) if t0 <= t < t1 and a <= UNIT * lo < b][0]
+            t0, t1, a, b = parts[n]
             engine.tensor_tensor(
                 units[:, lo:hi, t, :],
                 win[t][:, cells].rearrange("p (u c) -> p u c", c=UNIT),
-                skp[t // 2][:, t % 2, cells].rearrange("p (u c) -> p u c", c=UNIT),
+                skp[n][:, t - t0, UNIT * lo - a : UNIT * hi - a].rearrange("p (u c) -> p u c", c=UNIT),
                 ADD,
             )
 
-        for t in range(2):
-            for lo in (0, 4):
-                add(nc.gpsimd, t, lo, lo + 4)
+        for t, lo, hi in ((0, 0, 4), (0, 4, 8), (1, 0, 4), (1, 4, 6)):
+            add(nc.gpsimd, t, lo, hi)
         for lo, hi in STRETCHES:
+            if lo == 5:
+                add(nc.vector, 1, 6, 8)
             add(nc.vector, 2, lo, hi)
             add(nc.vector, 3, lo, hi)
 

from contextlib import ExitStack

import concourse.mybir as mybir

K, T, S, H, N, U = 1024, 2048, 512, 512, 128, 1024
FLOPS = 2 * K * H * S + 2 * H * N * U

F32 = mybir.dt.float32
BF16 = mybir.dt.bfloat16
I32 = mybir.dt.int32
U32 = mybir.dt.uint32
U16 = mybir.dt.uint16
U8 = mybir.dt.uint8
FP8X4 = mybir.dt.float8_e4m3fn_x4
FP4X4 = mybir.dt.float4_e2m1fn_x4
GELU = mybir.ActivationFunctionType.Gelu_apprx_tanh
COPY = mybir.ActivationFunctionType.Copy
ADD = mybir.AluOpType.add

P = 128
PASSES = K // 512
FIRST = 128
UNIT = 128
STRETCHES = ((0, 1), (1, 3), (3, 5), (5, 7), (7, 8))


def tile_picked_unet_gelu_p_kernel(
    tc, x_words, x_scales, w1, w2_words, w2_scales, skip, offs, cell, out
):
    nc = tc.nc
    with ExitStack() as ctx:
        lists = ctx.enter_context(tc.tile_pool(name="lists", bufs=1))
        sb = ctx.enter_context(tc.tile_pool(name="sb", bufs=1))
        ps = ctx.enter_context(tc.psum_pool(name="ps", bufs=1))

        def bank(b, name):
            return ps.tile([P, 512], F32, name=name, tag="bank%d" % b)

        def tile(shape, dtype, name, tag=None):
            return sb.tile(shape, dtype, name=name, tag=tag or name, align_bytes=64)

        offs_sb = lists.tile([P, S // 16], U16, name="offs_sb")
        cell_sb = lists.tile([P, S // 16], U16, name="cell_sb")
        xs = tile([P, T], U8, "xs")
        nc.gpsimd.memset(xs[:].bitcast(I32), 0)
        w2s = tile([P, N], U8, "w2s")
        nc.gpsimd.memset(w2s[:].bitcast(I32), 0)

        raw = [tile([P, 4, H], F32, "raw%d" % g) for g in range(PASSES)]
        xw = [tile([P, T], U32, "xw%d" % g) for g in range(PASSES)]
        parts = ((0, 1, 0, U), (1, 2, 0, 6 * UNIT), (2, 4, 0, U), (1, 2, 6 * UNIT, U))
        skp = [tile([P, t1 - t0, hi - lo], F32, "skip%d" % n) for n, (t0, t1, lo, hi) in enumerate(parts)]
        w2w = tile([P, 2 * N], U8, "w2w")

        def load_w(g):
            nc.sync.dma_start(raw[g][:], w1.rearrange("(g k j) c -> g k j c", g=PASSES, j=4)[g])

        def load_x(g):
            nc.sync.dma_start(xw[g][:].bitcast(I32), x_words[g].rearrange("p n t -> p (n t)").bitcast(I32))

        def load_scales(first, last):
            for r in range(first, last):
                g, q = divmod(r, 4)
                at = 32 * q + 4 * g
                nc.sync.dma_start(xs[at : at + 4, :].bitcast(I32), x_scales[g, 4 * q : 4 * q + 4, :].bitcast(I32))

        def load_skip(u):
            t0, t1, lo, hi = parts[u]
            nc.sync.dma_start(skp[u][:], skip.rearrange("(p t) v -> p t v", t=4)[:, t0:t1, lo:hi])

        load_w(0)
        nc.sync.dma_start(offs_sb[:], offs)
        nc.sync.dma_start(cell_sb[:], cell)
        load_scales(0, 3)
        load_x(0)
        load_scales(3, 8)
        load_w(1)
        load_x(1)
        load_skip(0)
        load_skip(1)
        nc.sync.dma_start(w2w[:].bitcast(I32), w2_words[0].bitcast(I32))
        for q in range(4):
            nc.sync.dma_start(
                w2s[32 * q : 32 * q + 4, :].bitcast(I32), w2_scales[0, 4 * q : 4 * q + 4, :].bitcast(I32)
            )
        load_skip(2)
        load_skip(3)

        win = [tile([P, U], F32, "win%d" % t) for t in range(4)]
        nc.vector.memset(win[0][:], 0.0)
        nc.scalar.activation(win[1][:], win[0][:], GELU)
        for t in (2, 3):
            nc.vector.memset(win[t][:], 0.0)

        sc, ve = nc.scalar.copy, nc.vector.tensor_copy

        def quant(src, name):
            words = src.shape[1] // 4
            codes = tile([P, words], U32, "c" + name)
            scales = tile([P, words], U8, "s" + name)
            nc.vector.quantize_mx(out=codes[:].bitcast(FP8X4), scales=scales[:], in_=src)
            return codes, scales

        def cast(copy, g, lo, hi):
            wb = tile([P, (hi - lo) * H], BF16, "wb%d%d" % (g, lo))
            copy(
                wb[:].rearrange("k (t m j) -> k m j t", m=P, j=4),
                raw[g][:].rearrange("k j (m t) -> k m j t", t=4)[:, :, :, lo:hi],
            )
            return wb

        wq = {}

        def quant_w(wb, g, lo, hi):
            codes, scales = quant(wb[:], "w%d%d" % (g, lo))
            for t in range(lo, hi):
                cols = slice(P * (t - lo), P * (t - lo + 1))
                wq[g, t] = (codes[:, cols], scales[:, cols])

        xsg = tile([P, S], U8, "xsg")
        xg = [tile([P, S], U32, "xg%d" % g) for g in range(PASSES)]
        quant_w(cast(sc, 0, 0, 4), 0, 0, 4)
        nc.vector.tensor_copy(xsg[:], xs[:].indirect(offs_sb[:]))
        nc.vector.tensor_copy(xg[0][:], xw[0][:].indirect(offs_sb[:]))
        early, late = cast(sc, 1, 0, 2), cast(ve, 1, 2, 4)
        quant_w(early, 1, 0, 2)
        quant_w(late, 1, 2, 4)
        nc.vector.tensor_copy(xg[1][:, :FIRST], xw[1][:].indirect(offs_sb[:, : FIRST // 16]))
        nc.vector.tensor_copy(xg[1][:, FIRST:], xw[1][:].indirect(offs_sb[:, FIRST // 16 :]))

        groups = [
            [(0, 0, FIRST), (1, 0, FIRST)],
            [(0, FIRST, 256), (0, 256, S)],
            [(1, FIRST, 256), (1, 256, S)],
            [(3, 0, S)],
            [(2, 0, S)],
        ]
        acc = [bank(b, "acc%d" % b) for b in range(len(groups) - 1)]

        def product(b, g):
            at = 0
            for i, (t, lo, hi) in enumerate(groups[b]):
                nc.tensor.matmul_mx(
                    out=acc[b][:, at : at + hi - lo],
                    lhsT=wq[g, t][0].bitcast(FP8X4),
                    lhsT_scale=wq[g, t][1],
                    rhs=xg[g][:, lo:hi].bitcast(FP8X4),
                    rhs_scale=xsg[4 * g : P, lo:hi],
                    start=(g == 0 and i == 0),
                    stop=(g == PASSES - 1 and i == len(groups[b]) - 1),
                )
                at = at + hi - lo

        for g in range(PASSES):
            for b in range(len(acc)):
                product(b, g)

        def gelu(b):
            width = sum(hi - lo for t, lo, hi in groups[b])
            h = tile([P, width], F32, "h%d" % b)
            nc.scalar.activation(h[:], acc[b][:, :width], GELU)
            return h

        def scatter_s(t, lo, hi, h):
            nc.scalar.activation(win[t][:].indirect(cell_sb[:, lo // 16 : hi // 16]), h, COPY)

        def scatter_v(t, lo, hi, h):
            nc.vector.tensor_copy(win[t][:].indirect(cell_sb[:, lo // 16 : hi // 16]), h)

        h = gelu(0)
        acc.append(bank(0, "acc4"))
        for g in range(PASSES):
            product(4, g)
        scatter_v(0, 0, FIRST, h[:, :FIRST])
        scatter_s(1, 0, FIRST, h[:, FIRST:])
        scatter_v(0, FIRST, S, gelu(1)[:])
        h1 = gelu(2)
        h3 = gelu(3)
        scatter_v(3, 0, FIRST, h3[:, :FIRST])
        h2 = gelu(4)
        scatter_s(1, FIRST, S, h1[:])
        scatter_v(2, 0, S, h2[:])
        scatter_s(3, FIRST, S, h3[:, FIRST:])

        planes = tile([P, 4 * U], BF16, "planes")
        units = planes[:].rearrange("p (u t c) -> p u t c", t=4, c=UNIT)

        def add(engine, t, lo, hi):
            cells = slice(UNIT * lo, UNIT * hi)
            n = [n for n, (t0, t1, a, b) in enumerate(parts) if t0 <= t < t1 and a <= UNIT * lo < b][0]
            t0, t1, a, b = parts[n]
            engine.tensor_tensor(
                units[:, lo:hi, t, :],
                win[t][:, cells].rearrange("p (u c) -> p u c", c=UNIT),
                skp[n][:, t - t0, UNIT * lo - a : UNIT * hi - a].rearrange("p (u c) -> p u c", c=UNIT),
                ADD,
            )

        for t, lo, hi in ((0, 0, 4), (0, 4, 8), (1, 0, 4), (1, 4, 6)):
            add(nc.gpsimd, t, lo, hi)
        for lo, hi in STRETCHES:
            if lo == 5:
                add(nc.vector, 1, 6, 8)
            add(nc.vector, 2, lo, hi)
            add(nc.vector, 3, lo, hi)

        def weave(copy, s):
            lo, hi = STRETCHES[s]
            z = tile([P, 4 * UNIT * (hi - lo)], BF16, "z%d" % s)
            copy(
                z[:].rearrange("p (u c i t) -> p u c t i", u=hi - lo, i=4, t=4),
                planes[:, 4 * UNIT * lo : 4 * UNIT * hi].rearrange("p (u t c i) -> p u c t i", u=hi - lo, t=4, i=4),
            )
            return z

        def finish(copy, s, z):
            codes, scales = quant(z[:], "z%d" % s)
            res = bank((4, 5, 6, 7, 1)[s], "res%d" % s)
            nc.tensor.matmul_mx(
                out=res[:, : codes.shape[1]],
                lhsT=w2w[:].bitcast(FP4X4),
                lhsT_scale=w2s[:],
                rhs=codes[:].bitcast(FP8X4),
                rhs_scale=scales[:],
                start=True,
                stop=True,
            )
            return res

        def store(copy, s, res):
            lo, hi = STRETCHES[s]
            o = tile([P, UNIT * (hi - lo)], F32, "o%d" % s)
            copy(o[:], res[:, : UNIT * (hi - lo)])
            nc.sync.dma_start(out[:, UNIT * lo : UNIT * hi], o[:])

        z0 = weave(sc, 0)
        z1 = weave(sc, 1)
        z2 = weave(sc, 2)
        z4 = weave(sc, 4)
        r0 = finish(sc, 0, z0)
        r1 = finish(sc, 1, z1)
        z3 = weave(ve, 3)
        r2 = finish(sc, 2, z2)
        r3 = finish(sc, 3, z3)
        r4 = finish(sc, 4, z4)
        store(sc, 0, r0)
        store(sc, 1, r1)
        store(sc, 2, r2)
        store(sc, 3, r3)
        store(ve, 4, r4)
